import numpy as np, ml_dtypes
CORES = [3,11,19,27,35,43,51,59]
N = 8
BF = ml_dtypes.bfloat16
def gentries(a):
    return np.ascontiguousarray(a.reshape(8, 16, -1).transpose(0, 2, 1)).reshape(8, -1)
def gtable(e):
    e = np.asarray(e); return np.ascontiguousarray(e.reshape(8, -1, 16).transpose(0, 2, 1)).reshape(128, -1).astype(np.int32)
T, C, R, S, VI = 2048, 4096, 32, 32, 5
def parts(rng):
    book = rng.integers(0, T, (N, 8, 16, C)); mix = rng.choice(np.array([0.2, 0.5, 0.8, 1.0]), (N, 8, 1, 1))
    W = np.minimum((256 * ((1 - mix) * rng.random((N, 8, 1, T)) + mix * rng.random((N, 8, 16, T)))).astype(np.int64), 255)
    wt = rng.integers(0, 256, (N, 8, 16)); sg = rng.integers(0, T, (N, 8, T)); sg[:, ::2] = np.argsort(rng.random((N, 4, T)), axis=-1)
    return book, W, wt, sg, rng.integers(0, C, (N, 8, S, R))
def pack(book, W, wt, sg, km):
    return {"book": np.ascontiguousarray(book.reshape(N, 128, C)).astype(np.int32), "tru": np.ascontiguousarray(W.reshape(N, 128, T)).astype(np.float32).astype(BF),
            "wt": np.ascontiguousarray(wt.reshape(N, 128, 1)).astype(np.int32), "sg0": np.stack([gtable(v) for v in sg]), "km0": np.stack([gtable(v.reshape(8, -1)) for v in km])}
def setup_inputs(rng):
    book, W, wt, sg, km = parts(rng)
    km[:, :, :, 3] = km[:, :, :1, 3]; km[:, :, :, 7] = km[:, :, :, 5]; km[:, :, :, 9] = km[:, :, :, 5]
    return pack(book, W, wt, sg, km)
def setup_inputs_spread(rng):
    book, W, wt, sg, km = parts(rng)
    W = np.minimum((np.exp2(8 * rng.random((N, 8, 1, T))) * rng.random((N, 8, 16, T)) * (rng.random((N, 8, 1, T)) > 0.0625)).astype(np.int64), 255)
    W[:, 1::2] = 255 - W[:, 1::2]; wt = np.minimum(np.exp2(8 * rng.random((N, 8, 16))).astype(np.int64), 255)
    book[:, :, ::2] = np.minimum((T * rng.random((N, 8, 8, C)) ** 3).astype(np.int64), T - 1)
    sg[:, ::3] = np.minimum((T * rng.random((N, 3, T)) ** 2).astype(np.int64), T - 1)
    km = np.minimum((C * rng.random((N, 8, S, R)) ** 2).astype(np.int64), C - 1)
    return pack(book, W, wt, sg, km)
def setup_inputs_ends(rng):
    book, W, wt, sg, km = parts(rng)
    kind = rng.random((N, 8, 1, T)); one = (np.arange(16)[:, None] == rng.integers(0, 16, (N, 8, 1, T))).astype(np.int64)
    bits = 255 * rng.integers(0, 2, (N, 8, 16, T))
    W = np.where(kind < 0.2, 255, np.where(kind < 0.32, 255 - one, np.where(kind < 0.44, 0, np.where(kind < 0.5, one, np.where(kind < 0.75, bits, W)))))
    sg = np.where(rng.random((N, 8, T)) < 0.65, (T - 1) * rng.integers(0, 2, (N, 8, T)), sg); sg[..., 0] = 0; sg[..., T - 1] = T - 1
    kc = rng.random((N, 8, 1, C)); two = (T - 1) * rng.integers(0, 2, (N, 8, 16, C))
    book = np.where(kc < 0.22, T - 1, np.where(kc < 0.33, 0, np.where(kc < 0.58, two, np.where((kc < 0.72) & (rng.random(book.shape) < 0.5), two, book))))
    book[..., 0] = (T - 1) * ((np.arange(16) + rng.integers(0, 2, (N, 8, 1))) % 2); book[..., C - 1] = T - 1
    km = np.where(rng.random(km.shape) < 0.65, (C - 1) * rng.integers(0, 2, km.shape), km)
    wt = 255 * rng.integers(0, 2, (N, 8, 16)); wt[:, :, :5] = rng.integers(0, 256, (N, 8, 5)); wt[:, 0] = 255; wt[:, 7] = 255; wt[:, 4] = 0
    for q in range(N):
        for g in range(8):
            kd = (g + q) % 4
            if q == N - 2 or (q == 0 and kd == 2) or (q == N - 1 and g == 7): kd = 0
            P = np.where(rng.permutation(16) < int(rng.integers(8, 10)), 255, 0)
            W[q, g, :, 0] = (0, 255, 255, 255 - P)[kd]; W[q, g, :, T - 1] = (255, 0, 255, P)[kd]
    km[0, :, 0, :] = 0
    km[N - 2, :, 0, :] = C - 1; km[N - 2, :, S - 1, :] = 0; km[N - 2, :, 1:S - 1, R - 1] = C - 1
    km[N - 1, 7, :, R - 1] = C - 1
    W[N - 1, 7, :, 7] = 255 * (np.arange(16) % 2); sg[N - 1, 7, 1] = 0; sg[N - 1, 7, 2] = 7; sg[N - 1, 7, T - 2] = T - 1
    e = np.full(16, 2); e[2] = T - 2; e[15] = T - 1; e[5] = 1; e[14] = 0; book[N - 1, 7, :, 600] = e
    return pack(book, W, wt, sg, km)
def setup_inputs_corners(rng):
    book, W, wt, sg, km = parts(rng); h = C // 2
    km[:, 0] = rng.integers(0, C, (N, 1, R))
    W[:, 1:3, :, :T // 2] = rng.integers(0, 100, (N, 2, 16, T // 2)); W[:, 1:3, :, T // 2:] = rng.integers(156, 256, (N, 2, 16, T - T // 2)); sg[:, 1:3] = np.arange(T)
    book[:, 1:3, :, :h] = rng.integers(T // 2, T, (N, 2, 16, h)); book[:, 1:3, :, h:] = rng.integers(0, T // 2, (N, 2, 16, C - h))
    km[:, 1] = rng.integers(0, h, (N, 1, R)); km[:, 1, S - 1] = rng.integers(h, C, (N, R))
    km[:, 2, 0] = rng.integers(0, h, (N, R)); km[:, 2, 1:] = rng.integers(h, C, (N, S - 1, R))
    book[:, 3, :, ::2] = rng.integers(0, T, (N, 1, h))
    sg[:, 4] = np.where(np.arange(T) % 2 == 0, 0, T - 1); book[:, 4] = (book[:, 4] // 2) * 2 + np.arange(C) % 2
    for q in range(N):
        m = 9 if q % 2 == 0 else 8
        W[q, 4, :, 0] = np.where(np.arange(16) < m, 10, 200); W[q, 4, :, T - 1] = np.where(np.arange(16) < m, 20, 100)
    wt[:, 5] = 0; wt[:, 7] = 255; wt[:, 6] = 255 * rng.integers(0, 2, (N, 16)); wt[:, 6, :4] = rng.integers(1, 256, (N, 4))
    few = np.concatenate([np.array([0, T - 1, 1, T - 2]), rng.permutation(T - 8)[:20] + 4]); book[:, 6] = few[book[:, 6] % 24]
    book[:, 7, 0] = T - 1; sg[:, 7, T - 1] = T - 1; W[:, 7, :, T - 1] = 255
    return pack(book, W, wt, sg, km)
def aim(rng, w, taken, m):
    V = rng.integers(0, 255, (16, 2048)); u = np.add.reduce(w[:, None] * V, axis=0) & 4095; n = ((u * u >> 5) + 37 * u) & (C - 1)
    v, i = np.unique(n, return_index=True); i = rng.permutation(i[~np.isin(v, taken)])[:m]
    return V[:, i], n[i]
def plant(rng, bk, Wg, s, cols, a, b, zero, top, rest, g):
    for j in range(R):
        kind = (j + g) % 3; one = (np.arange(16) == int(rng.integers(0, 16))).astype(np.int64); p, o = rng.permutation(16)[:2]
        pool = (rest, zero, top)[kind]; col = pool[rng.integers(0, len(pool), 16)]
        if kind == 1: p, o = int(rng.integers(1, 16)), 0
        if kind == 2: p, o = 0, int(rng.integers(1, 16))
        col[p] = a[j]; col[o] = b[j]; bk[:, cols[j]] = col
        Wg[:, s[a[j]]] = one if kind == 1 else 255
        Wg[:, s[b[j]]] = 255 - one if kind == 2 else 0
def setup_inputs_full(rng):
    book, W, wt, sg, km = parts(rng); W = np.clip(W, 1, 254); sg = np.argsort(rng.random((N, 8, T)), axis=-1); wt[:, :, 0] = 255
    for r in range(0, N - 1, 2):
        q = r + 1
        for g in range(8):
            x = rng.permutation(T); a0, b0, a1, b1 = np.array(x[:4 * R]).reshape(4, R)
            z, zero, top, rest = x[4 * R:5 * R + 1], x[5 * R + 1:5 * R + 17], x[5 * R + 17:5 * R + 33], x[5 * R + 33:]
            if g == 3: a1[7] = b0[7]; b1[9] = a0[9]
            if g == 5: a1[5] = a0[0]
            y = rng.permutation(C); O, P, X1, X = int(y[0]), int(y[1]), int(y[2]), y[3:3 + R]
            V0, n0 = aim(rng, wt[r, g], y[:3 + R], R); V1, n1 = aim(rng, wt[q, g], np.concatenate([y[:3], n0]), R + 1)
            for c in (r, q):
                W[c, g][:, sg[c, g][zero]] = 0; W[c, g][:, sg[c, g][top]] = 255
            W[r, g][:, sg[r, g][z[:R]]] = V0; book[r, g][:, X] = z[:R]; book[r, g][:, O] = zero[0]
            plant(rng, book[r, g], W[r, g], sg[r, g], n0, a0, b0, zero, top, rest, g)
            km[r, g, 0] = O; km[r, g, 1] = X
            W[q, g][:, sg[q, g][z]] = V1; book[q, g][:, n0] = z[:R]; book[q, g][:, X1] = z[R]
            book[q, g][:, O] = top[0]; book[q, g][:, P] = zero[0]; book[q, g][:, n1[R]] = top[1]
            plant(rng, book[q, g], W[q, g], sg[q, g], n1, a1, b1, zero, top, rest, g + 1)
            if g == 5: book[q, g][:, n1[0]] = a1[0]
            km[q, g, 0] = P; km[q, g, 1] = X1
    return pack(book, W, wt, sg, km)
def setup_inputs_hush(rng):
    book, W, wt, sg, km = parts(rng); q0 = int(rng.integers(0, N))
    for q in (q0, (q0 + 2) % N):
        for g in range(8):
            x = rng.permutation(T)[:3]; m = rng.permutation(T)[:3]; y = rng.permutation(C)[:3]
            hi = rng.integers(160, 255, 16) if g < 7 else np.where(rng.permutation(16) < 9, 254, 255)
            sg[q, g, x] = m; W[q, g, :, m[0]] = 0; W[q, g, :, m[1]] = 255; W[q, g, :, m[2]] = hi
            book[q, g] = np.where(book[q, g] == x[0], x[1], book[q, g]); book[q, g][:, y] = x
            wt[q, g] = rng.integers(224, 256, 16) if g < 7 else 255
            km[q, g, :, ::2] = y[1]; km[q, g, S - 1, ::2] = y[2]; km[(q - 1) % N, g, 0] = y[0]
    return pack(book, W, wt, sg, km)
def check_inputs(d):
    bad = []
    for k, lo, hi in (("book", 0, T - 1), ("tru", 0, 255), ("wt", 0, 255), ("sg0", 0, T - 1), ("km0", 0, C - 1)):
        v = np.asarray(d[k]).astype(np.float64)
        if not (np.min(v) >= lo and np.max(v) <= hi): bad.append("range of " + k)
        elif np.any(np.floor(v) != v): bad.append("whole numbers in " + k)
    return bad
def reference(book, tru, wt, sg0, km0):
    B = np.ascontiguousarray(book.astype(np.int64).reshape(N, 8, 16, C).transpose(0, 1, 3, 2))
    W = np.ascontiguousarray(tru.astype(np.float32).astype(np.int64).reshape(N, 8, 16, T).transpose(0, 1, 3, 2))
    w = wt.astype(np.int64).reshape(N, 8, 16)
    s = np.stack([gentries(v) for v in sg0]).astype(np.int64)
    K = np.stack([gentries(v) for v in km0]).astype(np.int64).reshape(N, 8, S, R)
    a = np.full((N, 8, S, R), -1, np.int64); b = np.full((N, 8, S, R), -1, np.int64)
    last = np.zeros(N, np.int64); ar = np.arange(R)
    for t in range(VI):
        new = np.zeros(N, np.int64)
        for r in range(N):
            q = (r + t) % N
            for g in range(8):
                Z = W[q, g][s[q, g]]
                y = np.min(Z[B[q, g][K[r, g].reshape(-1)]], axis=1).reshape(S, R, 16)
                con = np.add.reduce((y[1:] < y[:1]).astype(np.int64), axis=2) >= 9
                hit = np.any(con, axis=0); ks = np.where(hit, 1 + np.argmax(con, axis=0), 1 + t)
                u = np.add.reduce(y[ks, ar] * w[q, g], axis=1) & 4095
                n = ((u * u >> 5) + 37 * u + last[q]) & (C - 1)
                e = B[q, g][n]; sc = np.add.reduce(Z[e], axis=2)
                na = e[ar, np.argmax(sc, axis=1)]; nb = e[ar, np.argmin(sc, axis=1)]
                oa = np.where(hit, a[r, g, ks, ar], -1); ob = np.where(hit, b[r, g, ks, ar], -1)
                nm = np.stack([na, nb, oa, ob]); nm = np.where(nm < 0, T, nm)
                own = np.full(T + 1, R, np.int64); np.minimum.at(own, nm, np.broadcast_to(ar, (4, R))); own[T] = R
                ok = (na != nb) & (na != oa) & (na != ob) & (nb != oa) & (nb != ob) & ~np.any(own[nm] < ar, axis=0)
                old = np.array(s[q, g]); i = np.nonzero(ok)[0]; h = np.nonzero(ok & (oa >= 0))[0]
                s[q, g, na[i]] = old[nb[i]]; s[q, g, nb[i]] = old[na[i]]
                s[q, g, oa[h]] = old[ob[h]]; s[q, g, ob[h]] = old[oa[h]]
                K[r, g, ks, ar] = n; a[r, g, ks, ar] = np.where(ok, na, -1); b[r, g, ks, ar] = np.where(ok, nb, -1)
                new[q] += np.add.reduce(hit.astype(np.int64))
        last = new
    return {"yk": np.stack([gtable(v.reshape(8, -1)) for v in K]).astype(np.float32), "ya": np.stack([gtable(v.reshape(8, -1)) for v in a]).astype(np.float32),
            "yb": np.stack([gtable(v.reshape(8, -1)) for v in b]).astype(np.float32), "ys": s.astype(np.float32)}

@@ -1,0 +1,581 @@
+from concourse.bass import DstId, RemoteDMATransfer
+from concourse.mybir import AluOpType as A, AxisListType, ActivationFunctionType as AF
+
+SB = {
+    "bk": (4352, "int32"), "trs": (2048, "bfloat16"), "sgi": (128, "int32"), "kmi": (64, "int32"), "wti": (8, "int32"),
+    "Z": (2192, "bfloat16"), "SC": (2184, "float32"), "TW": (2056, "float32"), "SF": (2048, "float32"),
+    "IOS": (2048, "float32"), "HI": (2048, "bfloat16"), "LO": (2048, "bfloat16"),
+    "sgu": (128, "uint16"), "Kp": (64, "uint16"), "kmf": (64, "float32"), "KX": (512, "float32"),
+    "LP": (128, "uint16"), "E": (32, "uint16"), "NO": (2, "uint16"), "YL": (16, "uint16"), "KH": (2, "uint16"),
+    "SU": (8, "uint16"), "DU": (8, "uint16"), "MO": (32, "uint16"),
+    "GR": (16384, "bfloat16"), "Y": (16400, "bfloat16"), "GP": (2048, "bfloat16"), "YP": (2048, "bfloat16"),
+    "Y0": (32, "bfloat16"), "CM": (1024, "bfloat16"), "CP": (128, "bfloat16"), "KV": (64, "float32"), "KT": (64, "float32"), "RR": (2, "bfloat16"), "HN": (2, "bfloat16"),
+    "YS": (256, "bfloat16"), "SI": (2, "int32"), "UU": (2, "int32"), "VV": (2, "float32"), "PP": (2, "int32"), "N0": (2, "int32"),
+    "NI": (2, "int32"), "NJ": (2, "int32"), "CC": (1, "float32"), "TG": (512, "float32"), "KY": (512, "float32"), "KS": (512, "float32"),
+    "KI": (32, "int32"), "F": (32, "bfloat16"), "FX": (256, "bfloat16"), "O": (32, "bfloat16"), "OX": (256, "bfloat16"),
+    "NB": (128, "float16"), "LS": (16, "float32"), "EQ": (1024, "bfloat16"), "HS": (1024, "bfloat16"), "RM": (2, "float32"), "OK": (2, "float32"),
+    "TT": (8, "float32"), "DF": (8, "float32"), "ZT": (128, "bfloat16"), "ST": (128, "float32"), "DM": (32, "bfloat16"),
+    "OUT": (192, "float32"), "KE": (96, "float32"), "HV": (192, "float32"),
+    "D0": (2048, "bfloat16"), "KD": (256, "float32"), "HD": (1024, "bfloat16"), "IO": (128, "float32"), "IG": (128, "float32"), "IP": (128, "float32"),
+    "PI": (8, "int32"), "PF": (4, "float32"), "E16": (16, "float32"), "BO": (128, "bfloat16"), "BF4": (512, "float32"), "ID": (128, "bfloat16"), "P1": (128, "bfloat16"),
+    "P16": (128, "bfloat16"), "PD": (256, "bfloat16"), "G8": (8, "bfloat16"), "M8": (8, "float32"), "SG": (128, "bfloat16"), "EM": (256, "bfloat16"),
+    "EX": (128, "float32"), "CF": (16, "float32"), "CB": (16, "bfloat16"), "CA": (128, "bfloat16"), "CBB": (128, "bfloat16"), "ONE": (128, "bfloat16"),
+    "LC": (64, "uint16"), "LX": (16, "uint16"), "LK": (32, "uint16"), "L0": (8, "uint16"), "LT": (96, "float32"),
+    "T32": (32, "float32"), "Z32": (32, "float32"), "Q32": (32, "float32"), "THR": (2, "float32"), "DT": (8, "float32"), "BS1": (10, "bfloat16"), "BS2": (10, "bfloat16"),
+    "DH": (128, "bfloat16"), "DL": (128, "bfloat16"), "KC": (1, "float32"), "WB": (1, "bfloat16"), "IK": (96, "float32"),
+}
+MW = 48
+SCRATCH = {}
+PART = {}
+for _n in SB:
+    SCRATCH[_n] = ("sbuf", [128, SB[_n][0]], SB[_n][1])
+    PART[_n] = (_n, 0, SB[_n][0])
+
+
+def _parts(buf, names, w, dtype):
+    SCRATCH[buf] = ("sbuf", [128, w * len(names)], dtype)
+    for i, n in enumerate(names):
+        PART[n] = (buf, w * i, w)
+
+
+_parts("LBS", ["LB%d" % _t for _t in range(5)], 1024, "uint16")
+_parts("KINS", ["KIN%d" % _t for _t in range(1, 5)], 64, "uint16")
+_parts("NWS", ["NW%d" % _t for _t in range(1, 5)], 1056, "float32")
+_parts("MSS", ["MS%d" % _t for _t in range(5)] + ["ME"], MW, "float32")
+_parts("MGS", ["MG%d%d" % (_t, _v) for _t in range(1, 5) for _v in range(_t)], MW, "float32")
+_parts("HMS", ["HM%d" % _v for _v in range(1, 5)] + ["HE"], MW, "float32")
+for _b in range(8):
+    SCRATCH["p%d" % _b] = ("psum", [128, 512], "float32")
+    PART["p%d" % _b] = ("p%d" % _b, 0, 512)
+SEMAPHORES = ["cv", "cs", "ct", "cg", "loc"] + ["d%d" % _i for _i in range(16)] + ["k%d" % _i for _i in range(1, 5)] + \
+    ["m%d%d" % (_t, _v) for _t in range(1, 5) for _v in range(_t)] + ["h%d" % _v for _v in range(1, 5)] + ["he"]
+
+SCH = [4, 4, 4, 4, 4, 3, 1]
+VCH = [3, 3, 2]
+PLAN = ["g0", "S0", "V0", "g1", "S1", "V1", "S2", "pg", "g2", "L0", "L1", "V2", "S3", "L2", "L3", "S4", "ps", "S5", "S6"]
+NP = 3
+
+
+def rank_program(g, core, T, topo):
+    rank = T.rank_of(core)
+    if rank is None:
+        return
+    N = len(T.cores)
+    QU = {"v": g.vector, "s": g.scalar, "t": g.tensor, "g": g, "y": g.sync}
+    SEM = {"v": "cv", "s": "cs", "t": "ct", "g": "cg"}
+    cnt = {"cv": 0, "cs": 0, "ct": 0, "cg": 0}
+    known = {q: {} for q in QU}
+    vcs = {}
+    acc = {}
+    st = {"dma": 0, "loc": 0}
+
+    def need(q, tok):
+        sem, val = tok
+        if known[q].get(sem, 0) >= val:
+            return
+        QU[q].wait_ge(T.sem[sem], val)
+        kq = known[q]
+        for s2, v2 in vcs.get(tok, {}).items():
+            if kq.get(s2, 0) < v2:
+                kq[s2] = v2
+        kq[sem] = max(val, kq.get(sem, 0))
+
+    def deps(q, outs, ins):
+        ds = {}
+        for w, regs in ((True, outs), (False, ins)):
+            for (nm, lo, hi) in regs:
+                ps = nm[0] == "p"
+                for (l2, h2, w2, q2, tok) in acc.get(nm, ()):
+                    if ps and (q2 != q):
+                        hit = True
+                    elif ps and q == "t":
+                        hit = False
+                    else:
+                        hit = (w or w2) and l2 < hi and lo < h2
+                    if hit:
+                        ds[tok[0]] = max(ds.get(tok[0], 0), tok[1])
+        own = SEM.get(q)
+        for sem in sorted(ds, key=lambda s: (s == own, s)):
+            need(q, (sem, ds[sem]))
+
+    def record(q, tok, outs, ins):
+        v = dict(known[q])
+        v[tok[0]] = tok[1]
+        vcs[tok] = v
+        for w, regs in ((True, outs), (False, ins)):
+            for (nm, lo, hi) in regs:
+                old = acc.get(nm, [])
+                if w and nm[0] != "p":
+                    old = [r for r in old if not (lo <= r[0] and r[1] <= hi)]
+                else:
+                    old = [r for r in old if not (r[3] == q and r[2] == w and lo <= r[0] and r[1] <= hi and r[4][0] == tok[0])]
+                old.append((lo, hi, w, q, tok))
+                acc[nm] = old
+
+    def R(nm, lo=0, hi=None, step=1):
+        nm, off, wd = PART[nm]
+        lo, hi = lo + off, off + (wd if hi is None else hi)
+        return (T[nm][:, lo:hi] if step == 1 else T[nm][:, lo:hi:step], [(nm, lo, hi)])
+
+    def IND(win, off):
+        return (win[0].indirect(off[0]), win[1] + off[1])
+
+    def reg(x):
+        return x[1] if isinstance(x, tuple) else []
+
+    def ap(x):
+        return x[0] if isinstance(x, tuple) else x
+
+    def op(q, fn, outs, ins):
+        o = [r for x in outs for r in reg(x)]
+        i = [r for x in ins for r in reg(x)]
+        deps(q, o, i)
+        sem = SEM[q]
+        cnt[sem] += 1
+        fn().then_inc(T.sem[sem], 1)
+        record(q, (sem, cnt[sem]), o, i)
+
+    V, S, PE = g.vector, g.scalar, g.tensor
+
+    def cp(out, in_):
+        op("v", lambda: V.tensor_copy(ap(out), ap(in_)), [out], [in_])
+
+    def scatter(win, off, in_):
+        op("v", lambda: V.tensor_copy(win[0].indirect(off[0]), ap(in_)), [win], [in_, off])
+
+    def tt(out, a, b, o):
+        op("v", lambda: V.tensor_tensor(ap(out), ap(a), ap(b), o), [out], [a, b])
+
+    def ts(out, a, s1, o1, s2=None, o2=None):
+        if o2 is None:
+            op("v", lambda: V.tensor_scalar(ap(out), ap(a), ap(s1), None, o1), [out], [a, s1])
+        else:
+            op("v", lambda: V.tensor_scalar(ap(out), ap(a), ap(s1), ap(s2), o1, o2), [out], [a, s1, s2])
+
+    def ms(out, c):
+        op("v", lambda: V.memset(ap(out), c), [out], [])
+
+    def red(out, a, o):
+        op("v", lambda: V.tensor_reduce(ap(out), ap(a), AxisListType.X, o), [out], [a])
+
+    def scan(out, a, b, init, o1, o2):
+        op("v", lambda: V.tensor_tensor_scan(ap(out), ap(a), ap(b), init, o1, o2), [out], [a, b])
+
+    def act(out, a, **kw):
+        d = {k: ap(x) for k, x in kw.items()}
+        f = AF.Identity if "bias" in kw else AF.Copy
+        op("s", lambda: S.activation(ap(out), ap(a), f, **d), [out], [a] + list(kw.values()))
+
+    def ac(out, a, scale=1.0, bias=None):
+        if bias is None:
+            act(out, a, scale=scale)
+        else:
+            act(out, a, scale=scale, bias=bias)
+
+    def mm(out, l, r, start=True, stop=True):
+        op("t", lambda: PE.matmul(ap(out), ap(l), ap(r), start, stop), [out], [l, r])
+
+    def iota(out, pat, base=0, cm=0):
+        op("g", lambda: g.iota(ap(out), pat, base, cm, allow_small_or_imprecise_dtypes=True), [out], [])
+
+    def dma(q, oap, iap, outs, ins):
+        deps(q, outs, ins)
+        sem = "d%d" % st["dma"]
+        st["dma"] += 1
+        QU[q].dma_start(oap, iap).then_inc(T.sem[sem], 16)
+        record(q, (sem, 16), outs, ins)
+
+    def send(src, ws, dsts, first=False):
+        deps("g", [], R(src, 0, ws)[1])
+        if first:
+            send(src, ws, dsts[:1])
+            if len(dsts) > 1:
+                send(src, ws, dsts[1:])
+            return
+        k = 1
+        while k < len(dsts):
+            k *= 2
+        tr = []
+        for n, (r2, buf, sem) in enumerate(dsts):
+            c2 = T.cores[r2]
+            en = topo.engines(core, c2)
+            w = max(1, len(en) // k)
+            m = 0
+            for e in en[n * w:(n + 1) * w]:
+                m |= 1 << e
+            rid, pid, _se = topo.addr(c2)
+            tr.append(RemoteDMATransfer(dst_ids=[DstId(rid=rid, pnc=pid)], dma_engine_mask=m, remote_sem=T.sem[sem], src=R(src)[0], dst=R(buf)[0]))
+            st["loc"] += w
+        g.remote_dma_fused(tr, local_sem=T.sem["loc"])
+
+    def width(n):
+        k = 1
+        while k < n:
+            k *= 2
+        return max(1, len(topo.engines(T.cores[(rank + 1) % N], core)) // k)
+
+    def arrive(buf, sem, val):
+        (nm, lo, hi), = R(buf)[1]
+        acc.setdefault(nm, []).append((lo, hi, True, "r", (sem, val)))
+        vcs[(sem, val)] = {sem: val}
+
+    def dests(v, q):
+        r = (q - v) % N
+        d = [((r + t) % N, "MG%d%d" % (t, v), "m%d%d" % (t, v)) for t in range(v + 1, 5)]
+        if v:
+            d.append((r, "HM%d" % v, "h%d" % v))
+        return d
+
+    dma("s", T.sgi[:], T.sg0[:], [("sgi", 0, 128)], [])
+    dma("s", T.kmi[:], T.km0[:], [("kmi", 0, 64)], [])
+    dma("s", T.wti[:, 0:1], T.wt[:], [("wti", 0, 1)], [])
+    dma("y", T.trs[:], T.tru[:], [("trs", 0, 2048)], [])
+    dma("y", T.bk[:, 0:4096], T.book[:], [("bk", 0, 4096)], [])
+    dma("y", T.bk[:, 4096:4352], T.book[:, 0:256], [("bk", 4096, 4352)], [])
+
+    op("g", lambda: g.iota(T.PI[:, 0:1], [[0, 1]], 0, 1), [R("PI", 0, 1)], [])
+    iota(R("IO"), [[1, 128]])
+    iota(R("IG"), [[1, 8], [0, 16]])
+    iota(R("LT", 64, 96), [[32, 2], [1, 2], [0, 8]])
+    iota(R("LT", 0, 64), [[1, 32], [0, 2]])
+    iota(R("IP"), [[1, 8], [8, 4], [32, 4]])
+    iota(R("IOS"), [[1, 2048]])
+    iota(R("HI"), [[1, 64], [0, 32]])
+    iota(R("LO"), [[0, 64], [1, 32]])
+    ms(R("D0"), 0.0)
+    op("v", lambda: V.tensor_scalar(T.PI[:, 1:2], T.PI[:, 0:1], 15, None, A.bitwise_and), [R("PI", 1, 2)], [R("PI", 0, 1)])
+    op("v", lambda: V.tensor_scalar(T.PI[:, 2:3], T.PI[:, 0:1], 4, None, A.arith_shift_right), [R("PI", 2, 3)], [R("PI", 0, 1)])
+    op("v", lambda: V.tensor_scalar(T.PI[:, 3:4], T.PI[:, 0:1], 31, None, A.bitwise_and), [R("PI", 3, 4)], [R("PI", 0, 1)])
+    cp(R("PF", 0, 4), R("PI", 0, 4))
+    ts(R("E16"), R("IO", 0, 16), R("PF", 1, 2), A.is_equal)
+    ts(R("BO"), R("IG"), R("PF", 2, 3), A.is_equal)
+    ts(R("LT", 64, 96), R("LT", 64, 96), R("PF", 1, 2), A.add, R("PF", 1, 2), A.add)
+    cp(R("LK"), R("LT", 64, 96))
+    for i in range(4):
+        ts(R("BF4", 128 * i, 128 * i + 128), R("IG"), R("PF", 2, 3), A.is_equal)
+    ms(R("SG"), 0.0)
+    for i in range(4):
+        ac(R("SG", i, 128, 16), R("BO", i, 128, 16), 16.0 if i < 2 else -16.0)
+    cp(R("LC"), R("LT", 0, 64))
+    cp(R("sgu"), R("sgi"))
+    cp(R("kmf"), R("kmi"))
+    tt(R("KX"), IND(R("kmf"), R("LK")), R("BF4"), A.mult)
+    for i in range(4):
+        mm(R("p7", 16 * i, 16 * i + 16), R("KX", 128 * i, 128 * i + 128), R("E16"))
+    ms(R("D0", 0, 2048, 16), 256.0)
+    for kh in range(2):
+        cp(R("Kp", kh, 64, 2), R("p7", 32 * kh, 32 * kh + 32))
+    send("Kp", 64, [((rank + t) % N, "KIN%d" % t, "k%d" % t) for t in range(1, 5)])
+    for t in range(1, 5):
+        arrive("KIN%d" % t, "k%d" % t, width(4))
+    ms(R("Z", 0, 1), 0.0)
+    ms(R("Z", 2049, 2192), 0.0)
+    cp(R("Z", 1, 1025), IND(R("trs"), R("sgu", 0, 64)))
+    act(R("Z", 1025, 2049), IND(R("trs"), R("sgu", 64, 128)))
+    act(R("SF"), IND(R("IOS"), R("sgu")))
+    for t in range(1, 5):
+        iota(R("NW%d" % t), [[0, 1056]])
+    ms(R("KD"), 1.0)
+    ms(R("KD", 0, 256, 16), -1048576.0)
+    ms(R("HD"), 8.0)
+    ms(R("HD", 0, 1024, 32), 2.0 ** -93)
+    ms(R("HD", 0, 1024, 128), 0.0)
+    ts(R("P1"), R("IP"), R("PF", 0, 1), A.is_equal)
+    ts(R("ID"), R("IO"), R("PF", 0, 1), A.is_equal)
+    ts(R("M8"), R("IO", 0, 8), R("PF", 2, 3), A.is_equal)
+    ms(R("SC", 0, 1), 0.0)
+    ms(R("SC", 2049, 2184), 0.0)
+    for i in range(4):
+        mm(R("p%d" % i), R("SG"), R("Z", 1 + 512 * i, 513 + 512 * i))
+    for i in range(4):
+        act(R("SC", 1 + 512 * i, 513 + 512 * i), R("p%d" % i))
+    dma("y", T.SC[15:128:16, 1:2049], T.SF[15:128:16, :], [("SC", 0, 2052)], [("SF", 0, 2048)])
+
+    def lin(col, terms, frm=None):
+        prev = frm
+        for lane, val in terms:
+            if prev is None:
+                ac(R("CF", col, col + 1), R("E16", lane, lane + 1), float(val))
+            else:
+                ac(R("CF", col, col + 1), R("E16", lane, lane + 1), float(val), R("CF", prev, prev + 1))
+            prev = col
+    lin(13, [(0, 1), (2, 1)])
+    lin(14, [(1, 1), (3, 1)])
+    ac(R("DH"), R("ID"), R("CF", 13, 14))
+    ac(R("DL"), R("ID"), R("CF", 14, 15))
+    lin(12, [(0, -63.0 / 128), (1, -63.0 / 128), (2, -63.0 / 128), (3, -63.0 / 128), (4, 0.25), (5, 0.25), (7, 0.25)])
+    for i in range(4):
+        mm(R("p%d" % (3 + i)), R("DH"), R("HI", 512 * i, 512 * i + 512), True, False)
+        mm(R("p%d" % (3 + i)), R("DL"), R("LO", 512 * i, 512 * i + 512), False, True)
+    ms(R("TW", 0, 1), 0.0)
+    ms(R("TW", 2049, 2056), 0.0)
+
+    lin(0, [(0, 2048), (1, 64), (4, 4160), (5, 2)])
+    lin(1, [(2, 2048), (3, 64), (4, 4160), (5, 2)])
+    lin(10, [(0, 2048), (1, 64), (4, -4032), (5, -2), (7, -1)])
+    lin(11, [(2, 2048), (3, 64), (4, -4032), (5, -2), (7, -1)])
+    for b in range(2):
+        for nm in range(4):
+            q = 4 * b + nm
+            lin(2 + q, [(5, -4 * q)], frm=10 + nm % 2)
+    ac(R("CB", 0, 10), R("CF", 0, 10))
+    ac(R("CA"), R("BO"), R("CF", 0, 1))
+    ac(R("CBB"), R("BO"), R("CF", 1, 2))
+
+    def later():
+        for i in range(4):
+            act(R("TW", 1 + 512 * i, 513 + 512 * i), R("p%d" % (3 + i)), bias=R("CF", 12, 13), scale=1.0 / 64)
+    ac(R("P16"), R("P1"), 16.0)
+    ac(R("G8"), R("M8"))
+
+    ts(R("EX"), R("IG"), -16.0, A.mult)
+    tt(R("EX"), R("EX"), R("IO"), A.add)
+    ts(R("EX"), R("EX"), 32.0, A.mult, -1.0, A.add)
+    ts(R("EX"), R("EX"), R("E16", 7, 8), A.mult, 1.0, A.add)
+    for b in range(2):
+        tt(R("EM", 128 * b, 128 * b + 128), R("EX"), R("BF4", 0, 128), A.mult)
+    ts(R("Q32", 0, 2), R("IO", 0, 2), 16.0, A.mult, R("PF", 1, 2), A.add)
+    for i in range(4):
+        cp(R("L0", 2 * i, 2 * i + 2), R("Q32", 0, 2))
+    ts(R("LX", 0, 8), R("IG", 0, 8), 0.0, A.mult, R("PF", 1, 2), A.add)
+    ts(R("LX", 8, 16), R("IG", 0, 8), 16.0, A.add, R("PF", 1, 2), A.add)
+    for i, (m1, c1, m2, c2) in enumerate([(32, 32, 1, 0), (32, 32, 1, 0), (512, 512, 0, 31), (32, 32, 0, 0), (0, 32, 0, 0)]):
+        ts(R("BS1", 2 * i, 2 * i + 2), R("Q32", 0, 2), float(m1), A.mult, float(c1), A.add)
+        ts(R("BS2", 2 * i, 2 * i + 2), R("Q32", 0, 2), float(m2), A.mult, float(c2), A.add)
+    ms(R("T32"), 0.125)
+    ms(R("Z32"), 0.0)
+    scan(R("Q32"), R("T32"), R("Z32"), 1.75 * 2.0 ** 96, A.mult, A.add)
+    for b in range(2):
+        tt(R("T32", 16 * b, 16 * b + 16), R("Q32", 16 * b, 16 * b + 16), R("E16"), A.mult)
+        red(R("THR", b, b + 1), R("T32", 16 * b, 16 * b + 16), A.add)
+    ts(R("EX", 0, 1), R("PF", 1, 2), 8.0, A.mult, 2049.0, A.add)
+    ts(R("DT"), R("IO", 0, 8), R("EX", 0, 1), A.add)
+    ts(R("KC"), R("PF", 3, 4), -32.0, A.add)
+    cp(R("WB"), R("wti", 0, 1))
+    ms(R("Y", 0, 16), 0.0)
+    ms(R("O"), 0.0)
+    ms(R("OX"), 0.0)
+    ms(R("CC"), 0.0)
+    ms(R("ONE"), 1.0)
+    for t in range(5):
+        ms(R("MS%d" % t), 0.0)
+    ms(R("ME"), 0.0)
+    for i in range(3):
+        cp(R("IK", 32 * i, 32 * i + 32), R("IO", 0, 32))
+    cp(R("OUT", 0, 64), R("kmi"))
+    ms(R("OUT", 64, 192), -1.0)
+
+    def look(dst, c0, c1, lst):
+        ts(R(dst, c0, c1), IND(R("bk"), lst), 1.0, A.add)
+    for i in range(4):
+        look("LB0", 256 * i, 256 * i + 256, R("Kp", 16 * i, 16 * i + 16))
+
+    sj, j0 = [], 0
+    for n in SCH:
+        sj.append((j0, j0 + n))
+        j0 += n
+    vj = []
+    for n in VCH:
+        vj.append((j0, j0 + n))
+        j0 += n
+
+    for t in range(5):
+        L = "LB%d" % t
+        mst = "MS%d" % t
+        last = t == 4
+
+        pend = []
+
+        def least(a, b):
+            scan(R("Y", 16 + 512 * a, 16 + 512 * b), R("D0", 0, 512 * (b - a)), R("GR", 512 * a, 512 * b), 0.0, A.max, A.min)
+            compare()
+            cp(R("Y0", a, b), R("Y", 31 + 512 * a, 16 + 512 * b, 512))
+            pend.append((a, b))
+
+        def compare():
+            if not pend:
+                return
+            a, b = pend.pop()
+            tt(R("CM", 32 * a, 32 * b), IND(R("Y0", 0, b), R("LC", 2 * a, 2 * b)), R("Y", 31 + 512 * a, 16 + 512 * b, 16), A.is_gt)
+
+        def vec(w):
+            if w in ("pg", "ps"):
+                if w == "ps" and t:
+                    scan(R("YP", 0, 512 * t), R("D0", 0, 512 * t), R("GP", 0, 512 * t), 0.0, A.max, A.min)
+                return
+            i = int(w[1])
+            if w[0] == "L":
+                if not last:
+                    look("LB%d" % (t + 1), 256 * i, 256 * i + 256, R("KIN%d" % (t + 1), 16 * i, 16 * i + 16))
+                return
+            a, b = vj[i] if w[0] in "gV" else sj[i]
+            if w[0] == "g":
+                cp(R("GR", 512 * a, 512 * b), IND(R("Z"), R(L, 32 * a, 32 * b)))
+                compare()
+            else:
+                least(a, b)
+        for n, (a, b) in enumerate(sj):
+            if n == 5 and t:
+                act(R("GP", 0, 512 * t), IND(R("Z"), R("LP", 0, 32 * t)))
+            act(R("GR", 512 * a, 512 * b), IND(R("Z"), R(L, 32 * a, 32 * b)))
+            if n == NP - 1 and t:
+                for w in PLAN[:PLAN.index("pg")]:
+                    vec(w)
+                for v in range(t):
+                    arrive("MG%d%d" % (t, v), "m%d%d" % (t, v), width(1 if t == v + 1 else len(dests(v, 0)) - 1))
+                for v in range(t):
+                    cp(R("MO", 8 * v, 8 * v + 8), R("MG%d%d" % (t, v), 32, 40))
+                    look("LP", 32 * v, 32 * v + 32, R("MO", 8 * v, 8 * v + 2))
+                for v in range(t):
+                    scatter(R("NW%d" % t), R("MO", 8 * v + 2, 8 * v + 4), R("MG%d%d" % (t, v), 0, 32))
+        if not t:
+            later()
+        ac(R("PD", 128, 256), R("P1"), float(16 * (t - 31)))
+        ac(R("PD", 0, 128), R("P1"), float(t - 31))
+        for w in PLAN if not t else PLAN[PLAN.index("pg"):]:
+            vec(w)
+        compare()
+        if t:
+            tt(R("CP", 0, 32 * t), IND(R("Y0"), R("L0", 0, 2 * t)), R("YP", 15, 512 * t, 16), A.is_gt)
+        for v in range(t):
+            scatter(R("CM"), R("MO", 8 * v + 6, 8 * v + 8), R("CP", 32 * v, 32 * v + 32))
+        mm(R("p1", 0, 2), R("ID"), R("BS1", 4, 6), True, False)
+        mm(R("p1", 0, 2), R("ID"), R("BS2", 4, 6), False, False)
+        mm(R("p2", 0, 10), R("ID"), R("BS1"), True, False)
+        mm(R("p2", 0, 10), R("ID"), R("BS2"), False, False)
+        for c in range(8):
+            mm(R("p0", 8 * c, 8 * c + 8), R("CM", 128 * c, 128 * c + 128), R("G8"))
+        for v in range(t):
+            scatter(R("Y"), R("MO", 8 * v + 4, 8 * v + 6), R("YP", 512 * v + 15, 512 * v + 512, 16))
+        ts(R("KV"), R("p0", 0, 64), 8.5, A.is_ge, R("KC"), A.mult)
+        op("v", lambda: V.transpose(T.KT[:], T.KV[:]), [R("KT")], [R("KV")])
+        for b in range(2):
+            red(R("RR", b, b + 1), R("KT", 32 * b, 32 * b + 32), A.min)
+        ts(R("HN"), R("RR"), 0.0, A.is_equal)
+        d1 = R("PD", 0, 128)
+        d16 = R("PD", 128, 256)
+        mm(R("p1", 0, 2), R("P16"), R("RR"), False, False)
+        mm(R("p1", 0, 2), d16, R("HN"), False, True)
+        for i in (0, 1, 3, 4):
+            mm(R("p2", 2 * i, 2 * i + 2), R("P1"), R("RR"), False, False)
+        mm(R("p2", 4, 6), R("P16"), R("RR"), False, False)
+        for i in (1, 3, 4):
+            mm(R("p2", 2 * i, 2 * i + 2), d1, R("HN"), False, False)
+        mm(R("p2", 4, 6), d16, R("HN"), False, True)
+        if not last:
+            mm(R("p7", 0, 1), R("ONE"), R("HN", 0, 1), True, False)
+            mm(R("p7", 0, 1), R("ONE"), R("HN", 1, 2), False, True)
+        for b in range(2):
+            ts(R("YL", 8 * b, 8 * b + 8), R("M8"), R("p1", b, b + 1), A.mult)
+        act(R("YS", 128, 256), IND(R("Y"), R("YL", 8, 16)))
+        cp(R("YS", 0, 128), IND(R("Y"), R("YL", 0, 8)))
+        for b in range(2):
+            mm(R("p3", b, b + 1), R("YS", 128 * b, 128 * b + 128), R("WB"))
+        cp(R("KH"), R("p2", 0, 2))
+        if t:
+            act(R("O"), IND(R("NW%d" % t), R("KH")))
+        cp(R("SI"), R("p3", 0, 2))
+        op("v", lambda: V.tensor_scalar(T.UU[:], T.SI[:], 4095, None, A.bitwise_and), [R("UU")], [R("SI")])
+        ts(R("VV"), R("UU"), -2912.0, A.add)
+        for b in range(2):
+            ts(R("PP", b, b + 1), R("VV", b, b + 1), 7008.0, A.add, R("VV", b, b + 1), A.mult)
+        op("v", lambda: V.tensor_scalar(T.N0[:], T.PP[:], 5, 4095, A.arith_shift_right, A.bitwise_and), [R("N0")], [R("PP")])
+        ts(R("NO"), R("N0"), R("CC"), A.add)
+        look("E", 0, 32, R("NO"))
+        for h in range(2):
+            act(R("TG", 256 * h, 256 * h + 256), IND(R("TW"), R("E", 16 * h, 16 * h + 16)))
+        mm(R("p4", 64, 96), R("CA"), R("O"))
+        mm(R("p4", 96, 128), R("CBB"), R("O"))
+        if t:
+            tt(R("OX"), IND(R("O"), R("LX")), R("EM"), A.mult)
+        for b in range(2):
+            mm(R("p5", 4 * b + 2, 4 * b + 4), R("OX", 128 * b, 128 * b + 128), R("CB", 0, 2))
+            mm(R("p5", 4 * b + 10, 4 * b + 12), R("OX", 128 * b, 128 * b + 128), R("CB", 4 + 4 * b, 6 + 4 * b))
+        for h in range(2):
+            tt(R("KY", 256 * h, 256 * h + 256), IND(R("SC"), R("E", 16 * h, 16 * h + 16)), R("TG", 256 * h, 256 * h + 256), A.add)
+            scan(R("KS", 256 * h, 256 * h + 256), R("KD"), R("KY", 256 * h, 256 * h + 256), 0.0, A.add, A.max)
+        cp(R("KI"), R("KS", 15, 512, 16))
+        tt(R("F"), R("KS", 15, 512, 16), R("KI"), A.subtract)
+        mm(R("p4", 0, 32), R("CA"), R("F"))
+        mm(R("p4", 32, 64), R("CBB"), R("F"))
+        for b in range(2):
+            tt(R("FX", 128 * b, 128 * b + 128), IND(R("F"), R("LX", 8 * b, 8 * b + 8)), R("EM", 128 * b, 128 * b + 128), A.mult)
+            mm(R("p5", 4 * b, 4 * b + 2), R("FX", 128 * b, 128 * b + 128), R("CB", 0, 2))
+            mm(R("p5", 4 * b + 8, 4 * b + 10), R("FX", 128 * b, 128 * b + 128), R("CB", 2 + 4 * b, 4 + 4 * b))
+        ts(R("NB"), R("p4", 0, 128), 0.5, A.max)
+        ac(R("LS"), R("p5", 0, 16))
+        op("v", lambda: V.tensor_scalar(T.NI[:], T.N0[:], T.CC[:, 0:1], None, A.add), [R("NI")], [R("N0"), R("CC")])
+
+        def wrapped():
+            op("v", lambda: V.tensor_scalar(T.NJ[:], T.NI[:], 4095, None, A.bitwise_and), [R("NJ")], [R("NI")])
+            cp(R("ME" if last else mst, 32, 34), R("NJ"))
+        if last:
+            wrapped()
+            ac(R("ME", 44, 46), R("p2", 8, 10))
+            send("ME", MW, [((rank - 4) % N, "HE", "he")])
+        for i in range(8):
+            ts(R("EQ", 128 * i, 128 * i + 128), R("NB"), R("LS", i, i + 1), A.is_equal)
+        if not last:
+            ac(R(mst, 34, 40), R("p2", 2, 8))
+            ac(R(mst, 44, 46), R("p2", 8, 10))
+            ts(R("CC"), R("p7", 0, 1), -1.0, A.mult, 256.0, A.add)
+        scan(R("HS"), R("HD"), R("EQ"), 0.0, A.mult, A.add)
+        cp(R("SU", 0, 8, 2), R("LS", 1, 8, 2))
+        cp(R("SU", 1, 8, 2), R("LS", 0, 8, 2))
+        if not last:
+            act(R("ZT"), IND(R("Z"), R("SU")))
+        act(R("ST"), IND(R("SC"), R("SU")))
+        for b in range(2):
+            red(R("RM", b, b + 1), R("HS", 512 * b + 127, 512 * b + 512, 128), A.max)
+        tt(R("OK"), R("RM"), R("THR"), A.is_lt)
+        for b in range(2):
+            ts(R("TT", 4 * b, 4 * b + 4), R("LS", 8 + 4 * b, 12 + 4 * b), R("OK", b, b + 1), A.mult)
+        for b in range(2):
+            if not last:
+                ac(R("DM", 16 * b, 16 * b + 16), R("E16"), R("OK", b, b + 1))
+            ts(R(mst, 40 + 2 * b, 42 + 2 * b), R("LS", 4 * b, 4 * b + 2), R("OK", b, b + 1), A.mult, -1.0, A.add)
+        if last:
+            send(mst, MW, dests(t, rank), True)
+        else:
+            mm(R("p6", 0, 32), R("BO"), R("DM"))
+        tt(R("DF"), R("TT"), R("DT"), A.add)
+        cp(R("DU"), R("DF"))
+        if not last:
+            scatter(R("Z"), R("DU"), R("ZT"))
+            wrapped()
+            tt(R(mst, 0, 32), R("p6", 0, 32), R("F"), A.mult)
+            send(mst, MW, dests(t, rank), True)
+        scatter(R("SC"), R("DU"), R("ST"))
+
+    dma("y", T.ys[:], T.SC[15:128:16, 1:2049], [], [("SC", 1, 2049)])
+    arrive("HE", "he", width(1))
+    for v in range(5):
+        m = "HM%d" % v if v else "MS0"
+        if v:
+            arrive(m, "h%d" % v, width(1 if v == 4 else len(dests(v, 0)) - 1))
+        e = "HE" if v == 4 else m
+        for b in range(2):
+            k = R(e, 44 + b, 45 + b)
+            ts(R("KE"), R("IK"), k, A.not_equal)
+            tt(R("OUT", b, 192, 2), R("OUT", b, 192, 2), R("KE"), A.mult)
+            ts(R("HV", 96 * b, 96 * b + 32), R("IK", 0, 32), k, A.is_equal, R(e, 32 + b, 33 + b), A.mult)
+            if v == 4:
+                tt(R("OUT", b, 64, 2), R("OUT", b, 64, 2), R("HV", 96 * b, 96 * b + 32), A.add)
+        if v == 4:
+            dma("s", T.yk[:], T.OUT[:, 0:64], [], [("OUT", 0, 64)])
+        for b in range(2):
+            k = R(e, 44 + b, 45 + b)
+            for f in (1, 2):
+                ts(R("HV", 96 * b + 32 * f, 96 * b + 32 * f + 32), R("IK", 0, 32), k, A.is_equal, R(m, 39 + 2 * b + f, 40 + 2 * b + f), A.mult)
+            if v == 4:
+                tt(R("OUT", 64 + b, 192, 2), R("OUT", 64 + b, 192, 2), R("HV", 96 * b + 32, 96 * b + 96), A.add)
+            else:
+                tt(R("OUT", b, 192, 2), R("OUT", b, 192, 2), R("HV", 96 * b, 96 * b + 96), A.add)
+    dma("y", T.ya[:], T.OUT[:, 64:128], [], [("OUT", 64, 128)])
+    dma("s", T.yb[:], T.OUT[:, 128:192], [], [("OUT", 128, 192)])
+    for i in range(st["dma"]):
+        need("y", ("d%d" % i, 16))
+    g.wait_ge(T.sem["loc"], st["loc"])
+    need("g", ("cg", cnt["cg"]))
+    for q, s in (("v", "cv"), ("s", "cs"), ("t", "ct")):
+        need(q, (s, cnt[s]))

@@ -2,27 +2,28 @@ from concourse.bass import DstId, RemoteDMATransfer
 from concourse.mybir import AluOpType as A, AxisListType, ActivationFunctionType as AF
 
 SB = {
-    "bk": (4352, "int32"), "trs": (2048, "bfloat16"), "sgi": (128, "int32"), "kmi": (64, "int32"), "wti": (8, "int32"),
-    "Z": (2192, "bfloat16"), "SC": (2184, "float32"), "TW": (2056, "float32"), "SF": (2048, "float32"),
+    "bk": (5696, "int32"), "trs": (2048, "bfloat16"), "sgi": (128, "int32"), "kmi": (64, "int32"), "wti": (8, "int32"),
+    "Z": (2192, "bfloat16"), "SC": (2184, "float32"), "SF": (2048, "float32"),
     "IOS": (2048, "float32"), "HI": (2048, "bfloat16"), "LO": (2048, "bfloat16"),
     "sgu": (128, "uint16"), "Kp": (64, "uint16"), "kmf": (64, "float32"), "KX": (512, "float32"),
     "LP": (128, "uint16"), "E": (32, "uint16"), "NO": (2, "uint16"), "YL": (16, "uint16"), "KH": (2, "uint16"),
     "SU": (8, "uint16"), "DU": (8, "uint16"), "MO": (32, "uint16"),
     "GR": (16384, "bfloat16"), "Y": (16400, "bfloat16"), "GP": (2048, "bfloat16"), "YP": (2048, "bfloat16"),
-    "Y0": (32, "bfloat16"), "CM": (1024, "bfloat16"), "CP": (128, "bfloat16"), "KV": (64, "float32"), "KT": (64, "float32"), "RR": (2, "bfloat16"), "HN": (2, "bfloat16"),
-    "YS": (256, "bfloat16"), "SI": (2, "int32"), "UU": (2, "int32"), "VV": (2, "float32"), "PP": (2, "int32"), "N0": (2, "int32"),
-    "NI": (2, "int32"), "NJ": (2, "int32"), "CC": (1, "float32"), "TG": (512, "float32"), "KY": (512, "float32"), "KS": (512, "float32"),
+    "Y0": (32, "bfloat16"), "CM": (1024, "bfloat16"), "CP": (128, "bfloat16"), "KV": (64, "float32"), "KT": (64, "float32"),
+    "RR": (2, "bfloat16"), "HN": (2, "bfloat16"), "YS": (256, "bfloat16"), "SI": (2, "int32"), "C5": (1, "bfloat16"),
+    "VV": (2, "float32"), "PP": (2, "int32"), "N0": (2, "int32"),
+    "NI": (2, "int32"), "NJ": (2, "int32"), "CC": (1, "float32"), "SN": (128, "float32"), "KY": (512, "float32"), "KS": (512, "float32"),
     "KI": (32, "int32"), "F": (32, "bfloat16"), "FX": (256, "bfloat16"), "O": (32, "bfloat16"), "OX": (256, "bfloat16"),
     "NB": (128, "float16"), "LS": (16, "float32"), "EQ": (1024, "bfloat16"), "HS": (1024, "bfloat16"), "RM": (2, "float32"), "OK": (2, "float32"),
     "TT": (8, "float32"), "DF": (8, "float32"), "ZT": (128, "bfloat16"), "ST": (128, "float32"), "DM": (32, "bfloat16"),
-    "OUT": (192, "float32"), "KE": (96, "float32"), "HV": (192, "float32"),
+    "OUT": (128, "float32"), "KE": (64, "float32"), "HV": (128, "float32"), "AV": (2, "float32"), "AI": (192, "int32"), "OF": (128, "float32"),
     "D0": (2048, "bfloat16"), "KD": (256, "float32"), "HD": (1024, "bfloat16"), "IO": (128, "float32"), "IG": (128, "float32"), "IP": (128, "float32"),
     "PI": (8, "int32"), "PF": (4, "float32"), "E16": (16, "float32"), "BO": (128, "bfloat16"), "BF4": (512, "float32"), "ID": (128, "bfloat16"), "P1": (128, "bfloat16"),
     "P16": (128, "bfloat16"), "PD": (256, "bfloat16"), "G8": (8, "bfloat16"), "M8": (8, "float32"), "SG": (128, "bfloat16"), "EM": (256, "bfloat16"),
-    "EX": (128, "float32"), "CF": (16, "float32"), "CB": (16, "bfloat16"), "CA": (128, "bfloat16"), "CBB": (128, "bfloat16"), "ONE": (128, "bfloat16"),
+    "EX": (128, "float32"), "CF": (20, "float32"), "CB": (16, "bfloat16"), "CA": (128, "bfloat16"), "CBB": (128, "bfloat16"), "ONE": (128, "bfloat16"),
     "LC": (64, "uint16"), "LX": (16, "uint16"), "LK": (32, "uint16"), "L0": (8, "uint16"), "LT": (96, "float32"),
-    "T32": (32, "float32"), "Z32": (32, "float32"), "Q32": (32, "float32"), "THR": (2, "float32"), "DT": (8, "float32"), "BS1": (10, "bfloat16"), "BS2": (10, "bfloat16"),
-    "DH": (128, "bfloat16"), "DL": (128, "bfloat16"), "KC": (1, "float32"), "WB": (1, "bfloat16"), "IK": (96, "float32"),
+    "T32": (32, "float32"), "Z32": (32, "float32"), "Q32": (32, "float32"), "DT": (8, "float32"), "BS1": (10, "bfloat16"), "BS2": (10, "bfloat16"),
+    "TD": (256, "bfloat16"), "W2": (2, "float32"), "DH": (128, "bfloat16"), "DL": (128, "bfloat16"), "KC": (1, "float32"), "WB": (1, "bfloat16"), "IK": (32, "float32"),
 }
 MW = 48
 SCRATCH = {}
@@ -42,6 +43,7 @@ _parts("LBS", ["LB%d" % _t for _t in range(5)], 1024, "uint16")
 _parts("KINS", ["KIN%d" % _t for _t in range(1, 5)], 64, "uint16")
 _parts("NWS", ["NW%d" % _t for _t in range(1, 5)], 1056, "float32")
 _parts("MSS", ["MS%d" % _t for _t in range(5)] + ["ME"], MW, "float32")
+PART["MSS"] = ("MSS", 0, 6 * MW)
 _parts("MGS", ["MG%d%d" % (_t, _v) for _t in range(1, 5) for _v in range(_t)], MW, "float32")
 _parts("HMS", ["HM%d" % _v for _v in range(1, 5)] + ["HE"], MW, "float32")
 for _b in range(8):
@@ -83,15 +85,15 @@ def rank_program(g, core, T, topo):
     def deps(q, outs, ins):
         ds = {}
         for w, regs in ((True, outs), (False, ins)):
-            for (nm, lo, hi) in regs:
+            for (nm, lo, hi, sp) in regs:
                 ps = nm[0] == "p"
-                for (l2, h2, w2, q2, tok) in acc.get(nm, ()):
+                for (l2, h2, w2, q2, tok, s2) in acc.get(nm, ()):
                     if ps and (q2 != q):
                         hit = True
                     elif ps and q == "t":
                         hit = False
                     else:
-                        hit = (w or w2) and l2 < hi and lo < h2
+                        hit = (w or w2) and l2 < hi and lo < h2 and not (sp > 1 and sp == s2 and (lo - l2) % sp)
                     if hit:
                         ds[tok[0]] = max(ds.get(tok[0], 0), tok[1])
         own = SEM.get(q)
@@ -103,19 +105,22 @@ def rank_program(g, core, T, topo):
         v[tok[0]] = tok[1]
         vcs[tok] = v
         for w, regs in ((True, outs), (False, ins)):
-            for (nm, lo, hi) in regs:
+            for (nm, lo, hi, sp) in regs:
                 old = acc.get(nm, [])
+
+                def inside(r):
+                    return lo <= r[0] and r[1] <= hi and (sp == 1 or (sp == r[5] and (lo - r[0]) % sp == 0))
                 if w and nm[0] != "p":
-                    old = [r for r in old if not (lo <= r[0] and r[1] <= hi)]
+                    old = [r for r in old if not inside(r)]
                 else:
-                    old = [r for r in old if not (r[3] == q and r[2] == w and lo <= r[0] and r[1] <= hi and r[4][0] == tok[0])]
-                old.append((lo, hi, w, q, tok))
+                    old = [r for r in old if not (r[3] == q and r[2] == w and inside(r) and r[4][0] == tok[0])]
+                old.append((lo, hi, w, q, tok, sp))
                 acc[nm] = old
 
     def R(nm, lo=0, hi=None, step=1):
         nm, off, wd = PART[nm]
         lo, hi = lo + off, off + (wd if hi is None else hi)
-        return (T[nm][:, lo:hi] if step == 1 else T[nm][:, lo:hi:step], [(nm, lo, hi)])
+        return (T[nm][:, lo:hi] if step == 1 else T[nm][:, lo:hi:step], [(nm, lo, hi, step)])
 
     def IND(win, off):
         return (win[0].indirect(off[0]), win[1] + off[1])
@@ -152,6 +157,12 @@ def rank_program(g, core, T, topo):
         else:
             op("v", lambda: V.tensor_scalar(ap(out), ap(a), ap(s1), ap(s2), o1, o2), [out], [a, s1, s2])
 
+    def bits(out, a, s1, o1, s2=None, o2=None):
+        if o2 is None:
+            op("v", lambda: V.tensor_scalar(ap(out), ap(a), s1, None, o1), [out], [a])
+        else:
+            op("v", lambda: V.tensor_scalar(ap(out), ap(a), s1, s2, o1, o2), [out], [a])
+
     def ms(out, c):
         op("v", lambda: V.memset(ap(out), c), [out], [])
 
@@ -179,6 +190,7 @@ def rank_program(g, core, T, topo):
         op("g", lambda: g.iota(ap(out), pat, base, cm, allow_small_or_imprecise_dtypes=True), [out], [])
 
     def dma(q, oap, iap, outs, ins):
+        outs, ins = [x + (1,) for x in outs], [x + (1,) for x in ins]
         deps(q, outs, ins)
         sem = "d%d" % st["dma"]
         st["dma"] += 1
@@ -215,8 +227,8 @@ def rank_program(g, core, T, topo):
         return max(1, len(topo.engines(T.cores[(rank + 1) % N], core)) // k)
 
     def arrive(buf, sem, val):
-        (nm, lo, hi), = R(buf)[1]
-        acc.setdefault(nm, []).append((lo, hi, True, "r", (sem, val)))
+        (nm, lo, hi, _sp), = R(buf)[1]
+        acc.setdefault(nm, []).append((lo, hi, True, "r", (sem, val), 1))
         vcs[(sem, val)] = {sem: val}
 
     def dests(v, q):
@@ -231,7 +243,7 @@ def rank_program(g, core, T, topo):
     dma("s", T.wti[:, 0:1], T.wt[:], [("wti", 0, 1)], [])
     dma("y", T.trs[:], T.tru[:], [("trs", 0, 2048)], [])
     dma("y", T.bk[:, 0:4096], T.book[:], [("bk", 0, 4096)], [])
-    dma("y", T.bk[:, 4096:4352], T.book[:, 0:256], [("bk", 4096, 4352)], [])
+    dma("y", T.bk[:, 4096:5696], T.book[:, 0:1600], [("bk", 4096, 5696)], [])
 
     op("g", lambda: g.iota(T.PI[:, 0:1], [[0, 1]], 0, 1), [R("PI", 0, 1)], [])
     iota(R("IO"), [[1, 128]])
@@ -239,21 +251,24 @@ def rank_program(g, core, T, topo):
     iota(R("LT", 64, 96), [[32, 2], [1, 2], [0, 8]])
     iota(R("LT", 0, 64), [[1, 32], [0, 2]])
     iota(R("IP"), [[1, 8], [8, 4], [32, 4]])
-    iota(R("IOS"), [[1, 2048]])
+    iota(R("IK"), [[1, 32]])
     iota(R("HI"), [[1, 64], [0, 32]])
     iota(R("LO"), [[0, 64], [1, 32]])
+    iota(R("IOS"), [[1, 2048]])
     ms(R("D0"), 0.0)
-    op("v", lambda: V.tensor_scalar(T.PI[:, 1:2], T.PI[:, 0:1], 15, None, A.bitwise_and), [R("PI", 1, 2)], [R("PI", 0, 1)])
-    op("v", lambda: V.tensor_scalar(T.PI[:, 2:3], T.PI[:, 0:1], 4, None, A.arith_shift_right), [R("PI", 2, 3)], [R("PI", 0, 1)])
-    op("v", lambda: V.tensor_scalar(T.PI[:, 3:4], T.PI[:, 0:1], 31, None, A.bitwise_and), [R("PI", 3, 4)], [R("PI", 0, 1)])
+    bits(R("PI", 1, 2), R("PI", 0, 1), 15, A.bitwise_and)
+    bits(R("PI", 2, 3), R("PI", 0, 1), 4, A.arith_shift_right)
+    bits(R("PI", 3, 4), R("PI", 0, 1), 31, A.bitwise_and)
     cp(R("PF", 0, 4), R("PI", 0, 4))
     ts(R("E16"), R("IO", 0, 16), R("PF", 1, 2), A.is_equal)
+    ts(R("ID"), R("IO"), R("PF", 0, 1), A.is_equal)
     ts(R("BO"), R("IG"), R("PF", 2, 3), A.is_equal)
     ts(R("LT", 64, 96), R("LT", 64, 96), R("PF", 1, 2), A.add, R("PF", 1, 2), A.add)
     cp(R("LK"), R("LT", 64, 96))
     for i in range(4):
         ts(R("BF4", 128 * i, 128 * i + 128), R("IG"), R("PF", 2, 3), A.is_equal)
     ms(R("SG"), 0.0)
+    ms(R("TD"), 0.0)
     for i in range(4):
         ac(R("SG", i, 128, 16), R("BO", i, 128, 16), 16.0 if i < 2 else -16.0)
     cp(R("LC"), R("LT", 0, 64))
@@ -270,9 +285,37 @@ def rank_program(g, core, T, topo):
         arrive("KIN%d" % t, "k%d" % t, width(4))
     ms(R("Z", 0, 1), 0.0)
     ms(R("Z", 2049, 2192), 0.0)
+
+    def lin(*cols):
+        prev = {c: f for c, _t, f in cols}
+        for n in range(max(len(tm) for _c, tm, _f in cols)):
+            for c, tm, _f in cols:
+                if n < len(tm):
+                    lane, val = tm[n]
+                    if prev[c] is None:
+                        ac(R("CF", c, c + 1), R("E16", lane, lane + 1), float(val))
+                    else:
+                        ac(R("CF", c, c + 1), R("E16", lane, lane + 1), float(val), R("CF", prev[c], prev[c] + 1))
+                    prev[c] = c
+    K = 1.0 / 32768
+    lin((13, [(0, 1.0 / 64), (2, 1.0 / 64)], None), (14, [(1, 1.0 / 64), (3, 1.0 / 64)], None),
+        (12, [(0, -63.0 / 128), (1, -63.0 / 128), (2, -63.0 / 128), (3, -63.0 / 128), (4, 0.25), (5, 0.25), (7, 0.25)], None),
+        (0, [(0, 2048), (1, 64), (4, 4160), (5, 2)], None), (1, [(2, 2048), (3, 64), (4, 4160), (5, 2)], None),
+        (10, [(0, 2048 * K), (1, 64 * K), (4, -4032 * K), (5, -2 * K), (7, -K)], None),
+        (11, [(2, 2048 * K), (3, 64 * K), (4, -4032 * K), (5, -2 * K), (7, -K)], None),
+        (15, [(0, 1), (2, -1)], None), (16, [(0, -1), (2, 1)], None), (17, [(1, 1), (3, -1)], None), (18, [(1, -1), (3, 1)], None))
+    ac(R("DH"), R("ID"), R("CF", 13, 14))
+    ac(R("DL"), R("ID"), R("CF", 14, 15))
+    lin(*[(2 + q, [(5, -4 * q * K)], 10 + q % 2) for q in range(8)])
+    ac(R("CB", 0, 10), R("CF", 0, 10))
+    ac(R("CA"), R("BO"), R("CF", 0, 1))
+    ac(R("CBB"), R("BO"), R("CF", 1, 2))
+    for i in range(2):
+        for l in (i, i + 2):
+            for sg in range(2):
+                ac(R("TD", 128 * sg + l, 128 * sg + 128, 16), R("BO", i, 128, 16), R("CF", 15 + 2 * i + sg, 16 + 2 * i + sg))
     cp(R("Z", 1, 1025), IND(R("trs"), R("sgu", 0, 64)))
     act(R("Z", 1025, 2049), IND(R("trs"), R("sgu", 64, 128)))
-    act(R("SF"), IND(R("IOS"), R("sgu")))
     for t in range(1, 5):
         iota(R("NW%d" % t), [[0, 1056]])
     ms(R("KD"), 1.0)
@@ -281,53 +324,17 @@ def rank_program(g, core, T, topo):
     ms(R("HD", 0, 1024, 32), 2.0 ** -93)
     ms(R("HD", 0, 1024, 128), 0.0)
     ts(R("P1"), R("IP"), R("PF", 0, 1), A.is_equal)
-    ts(R("ID"), R("IO"), R("PF", 0, 1), A.is_equal)
     ts(R("M8"), R("IO", 0, 8), R("PF", 2, 3), A.is_equal)
     ms(R("SC", 0, 1), 0.0)
     ms(R("SC", 2049, 2184), 0.0)
-    for i in range(4):
-        mm(R("p%d" % i), R("SG"), R("Z", 1 + 512 * i, 513 + 512 * i))
-    for i in range(4):
-        act(R("SC", 1 + 512 * i, 513 + 512 * i), R("p%d" % i))
-    dma("y", T.SC[15:128:16, 1:2049], T.SF[15:128:16, :], [("SC", 0, 2052)], [("SF", 0, 2048)])
-
-    def lin(col, terms, frm=None):
-        prev = frm
-        for lane, val in terms:
-            if prev is None:
-                ac(R("CF", col, col + 1), R("E16", lane, lane + 1), float(val))
-            else:
-                ac(R("CF", col, col + 1), R("E16", lane, lane + 1), float(val), R("CF", prev, prev + 1))
-            prev = col
-    lin(13, [(0, 1), (2, 1)])
-    lin(14, [(1, 1), (3, 1)])
-    ac(R("DH"), R("ID"), R("CF", 13, 14))
-    ac(R("DL"), R("ID"), R("CF", 14, 15))
-    lin(12, [(0, -63.0 / 128), (1, -63.0 / 128), (2, -63.0 / 128), (3, -63.0 / 128), (4, 0.25), (5, 0.25), (7, 0.25)])
-    for i in range(4):
-        mm(R("p%d" % (3 + i)), R("DH"), R("HI", 512 * i, 512 * i + 512), True, False)
-        mm(R("p%d" % (3 + i)), R("DL"), R("LO", 512 * i, 512 * i + 512), False, True)
-    ms(R("TW", 0, 1), 0.0)
-    ms(R("TW", 2049, 2056), 0.0)
-
-    lin(0, [(0, 2048), (1, 64), (4, 4160), (5, 2)])
-    lin(1, [(2, 2048), (3, 64), (4, 4160), (5, 2)])
-    lin(10, [(0, 2048), (1, 64), (4, -4032), (5, -2), (7, -1)])
-    lin(11, [(2, 2048), (3, 64), (4, -4032), (5, -2), (7, -1)])
-    for b in range(2):
-        for nm in range(4):
-            q = 4 * b + nm
-            lin(2 + q, [(5, -4 * q)], frm=10 + nm % 2)
-    ac(R("CB", 0, 10), R("CF", 0, 10))
-    ac(R("CA"), R("BO"), R("CF", 0, 1))
-    ac(R("CBB"), R("BO"), R("CF", 1, 2))
-
-    def later():
-        for i in range(4):
-            act(R("TW", 1 + 512 * i, 513 + 512 * i), R("p%d" % (3 + i)), bias=R("CF", 12, 13), scale=1.0 / 64)
     ac(R("P16"), R("P1"), 16.0)
     ac(R("G8"), R("M8"))
-
+    for i in range(4):
+        mm(R("p%d" % i), R("SG"), R("Z", 1 + 512 * i, 513 + 512 * i), True, False)
+        mm(R("p%d" % i), R("DH"), R("HI", 512 * i, 512 * i + 512), False, False)
+        mm(R("p%d" % i), R("DL"), R("LO", 512 * i, 512 * i + 512), False, True)
+    for i in range(4):
+        act(R("SC", 1 + 512 * i, 513 + 512 * i), R("p%d" % i), bias=R("CF", 12, 13))
     ts(R("EX"), R("IG"), -16.0, A.mult)
     tt(R("EX"), R("EX"), R("IO"), A.add)
     ts(R("EX"), R("EX"), 32.0, A.mult, -1.0, A.add)
@@ -342,33 +349,62 @@ def rank_program(g, core, T, topo):
     for i, (m1, c1, m2, c2) in enumerate([(32, 32, 1, 0), (32, 32, 1, 0), (512, 512, 0, 31), (32, 32, 0, 0), (0, 32, 0, 0)]):
         ts(R("BS1", 2 * i, 2 * i + 2), R("Q32", 0, 2), float(m1), A.mult, float(c1), A.add)
         ts(R("BS2", 2 * i, 2 * i + 2), R("Q32", 0, 2), float(m2), A.mult, float(c2), A.add)
-    ms(R("T32"), 0.125)
+    ms(R("T32"), 8.0)
     ms(R("Z32"), 0.0)
-    scan(R("Q32"), R("T32"), R("Z32"), 1.75 * 2.0 ** 96, A.mult, A.add)
+    scan(R("Q32"), R("T32"), R("Z32"), 2.0 ** -96, A.mult, A.add)
     for b in range(2):
         tt(R("T32", 16 * b, 16 * b + 16), R("Q32", 16 * b, 16 * b + 16), R("E16"), A.mult)
-        red(R("THR", b, b + 1), R("T32", 16 * b, 16 * b + 16), A.add)
+        red(R("W2", b, b + 1), R("T32", 16 * b, 16 * b + 16), A.add)
     ts(R("EX", 0, 1), R("PF", 1, 2), 8.0, A.mult, 2049.0, A.add)
-    ts(R("DT"), R("IO", 0, 8), R("EX", 0, 1), A.add)
+    ts(R("DT"), R("IO", 0, 8), R("EX", 0, 1), A.add, K, A.mult)
     ts(R("KC"), R("PF", 3, 4), -32.0, A.add)
     cp(R("WB"), R("wti", 0, 1))
     ms(R("Y", 0, 16), 0.0)
     ms(R("O"), 0.0)
     ms(R("OX"), 0.0)
-    ms(R("CC"), 0.0)
+    ms(R("CC"), 1336.0)
+    ms(R("C5"), 592.0)
     ms(R("ONE"), 1.0)
-    for t in range(5):
-        ms(R("MS%d" % t), 0.0)
-    ms(R("ME"), 0.0)
-    for i in range(3):
-        cp(R("IK", 32 * i, 32 * i + 32), R("IO", 0, 32))
+    ms(R("MSS"), 0.0)
     cp(R("OUT", 0, 64), R("kmi"))
-    ms(R("OUT", 64, 192), -1.0)
+    ms(R("OUT", 64, 128), -4097.0)
 
     def look(dst, c0, c1, lst):
         ts(R(dst, c0, c1), IND(R("bk"), lst), 1.0, A.add)
     for i in range(4):
         look("LB0", 256 * i, 256 * i + 256, R("Kp", 16 * i, 16 * i + 16))
+
+    fillers = []
+
+    def fill(n=1):
+        for _i in range(n):
+            if fillers:
+                fillers.pop(0)()
+
+    def go(f, *a):
+        fillers.append(lambda: f(*a))
+
+    def home(m):
+        for b in range(2):
+            go(ts, R("AV", b, b + 1), R(m, 40 + 2 * b, 41 + 2 * b), 4096.0, A.mult, R(m, 41 + 2 * b, 42 + 2 * b), A.add)
+            go(ts, R("KE", 32 * b, 32 * b + 32), R("IK"), R(m, 44 + b, 45 + b), A.not_equal)
+        for f in range(2):
+            for b in range(2):
+                o = R("OUT", 64 * f + b, 64 * f + 64, 2)
+                go(tt, o, o, R("KE", 32 * b, 32 * b + 32), A.mult)
+        for f in range(2):
+            for b in range(2):
+                go(ts, R("HV", 64 * f + b, 64 * f + 64, 2), R("IK"), R(m, 44 + b, 45 + b), A.is_equal, R("AV", b, b + 1) if f else R(m, 32 + b, 33 + b), A.mult)
+        for f in range(2):
+            o = R("OUT", 64 * f, 64 * f + 64)
+            go(tt, o, o, R("HV", 64 * f, 64 * f + 64), A.add)
+
+    def apart():
+        go(ts, R("AI", 0, 64), R("OUT", 64, 128), 4097.0, A.add)
+        go(bits, R("AI", 64, 128), R("AI", 0, 64), 12, A.arith_shift_right)
+        go(bits, R("AI", 128, 192), R("AI", 0, 64), 4095, A.bitwise_and)
+        go(ts, R("OF", 0, 64), R("AI", 64, 128), -1.0, A.add)
+        go(ts, R("OF", 64, 128), R("AI", 128, 192), -1.0, A.add)
 
     sj, j0 = [], 0
     for n in SCH:
@@ -383,20 +419,23 @@ def rank_program(g, core, T, topo):
         L = "LB%d" % t
         mst = "MS%d" % t
         last = t == 4
-
-        pend = []
+        pend, pend0 = [], []
 
         def least(a, b):
             scan(R("Y", 16 + 512 * a, 16 + 512 * b), R("D0", 0, 512 * (b - a)), R("GR", 512 * a, 512 * b), 0.0, A.max, A.min)
             compare()
-            cp(R("Y0", a, b), R("Y", 31 + 512 * a, 16 + 512 * b, 512))
-            pend.append((a, b))
+            pend0.append((a, b))
 
         def compare():
-            if not pend:
-                return
-            a, b = pend.pop()
-            tt(R("CM", 32 * a, 32 * b), IND(R("Y0", 0, b), R("LC", 2 * a, 2 * b)), R("Y", 31 + 512 * a, 16 + 512 * b, 16), A.is_gt)
+            first = pend0.pop(0) if pend0 else None
+            if first:
+                a, b = first
+                cp(R("Y0", a, b), R("Y", 31 + 512 * a, 16 + 512 * b, 512))
+            if pend:
+                a, b = pend.pop(0)
+                tt(R("CM", 32 * a, 32 * b), IND(R("Y0", 0, b), R("LC", 2 * a, 2 * b)), R("Y", 31 + 512 * a, 16 + 512 * b, 16), A.is_gt)
+            if first:
+                pend.append(first)
 
         def vec(w):
             if w in ("pg", "ps"):
@@ -429,34 +468,48 @@ def rank_program(g, core, T, topo):
                 for v in range(t):
                     scatter(R("NW%d" % t), R("MO", 8 * v + 2, 8 * v + 4), R("MG%d%d" % (t, v), 0, 32))
         if not t:
-            later()
+            act(R("SF"), IND(R("IOS"), R("sgu")))
+            dma("y", T.SC[15:128:16, 1:2049], T.SF[15:128:16, :], [("SC", 0, 2052)], [("SF", 0, 2048)])
         ac(R("PD", 128, 256), R("P1"), float(16 * (t - 31)))
         ac(R("PD", 0, 128), R("P1"), float(t - 31))
         for w in PLAN if not t else PLAN[PLAN.index("pg"):]:
             vec(w)
         compare()
+        compare()
         if t:
             tt(R("CP", 0, 32 * t), IND(R("Y0"), R("L0", 0, 2 * t)), R("YP", 15, 512 * t, 16), A.is_gt)
         for v in range(t):
             scatter(R("CM"), R("MO", 8 * v + 6, 8 * v + 8), R("CP", 32 * v, 32 * v + 32))
+        if t:
+            if t > 1:
+                arrive("HM%d" % (t - 1), "h%d" % (t - 1), width(len(dests(t - 1, 0)) - 1))
+            home("HM%d" % (t - 1) if t > 1 else "MS0")
+        if last:
+            apart()
         mm(R("p1", 0, 2), R("ID"), R("BS1", 4, 6), True, False)
         mm(R("p1", 0, 2), R("ID"), R("BS2", 4, 6), False, False)
         mm(R("p2", 0, 10), R("ID"), R("BS1"), True, False)
         mm(R("p2", 0, 10), R("ID"), R("BS2"), False, False)
+        mm(R("p6", 0, 2), R("ID"), R("BS1", 0, 2), True, False)
+        mm(R("p6", 0, 2), R("ID"), R("BS2", 0, 2), False, False)
         for c in range(8):
             mm(R("p0", 8 * c, 8 * c + 8), R("CM", 128 * c, 128 * c + 128), R("G8"))
         for v in range(t):
             scatter(R("Y"), R("MO", 8 * v + 4, 8 * v + 6), R("YP", 512 * v + 15, 512 * v + 512, 16))
         ts(R("KV"), R("p0", 0, 64), 8.5, A.is_ge, R("KC"), A.mult)
+        fill()
         op("v", lambda: V.transpose(T.KT[:], T.KV[:]), [R("KT")], [R("KV")])
+        fill()
         for b in range(2):
             red(R("RR", b, b + 1), R("KT", 32 * b, 32 * b + 32), A.min)
+        fill()
+        mm(R("p1", 0, 2), R("P16"), R("RR"), False, False)
+        mm(R("p6", 0, 2), R("P1"), R("RR"), False, True)
         ts(R("HN"), R("RR"), 0.0, A.is_equal)
         d1 = R("PD", 0, 128)
         d16 = R("PD", 128, 256)
-        mm(R("p1", 0, 2), R("P16"), R("RR"), False, False)
         mm(R("p1", 0, 2), d16, R("HN"), False, True)
-        for i in (0, 1, 3, 4):
+        for i in (1, 3, 4):
             mm(R("p2", 2 * i, 2 * i + 2), R("P1"), R("RR"), False, False)
         mm(R("p2", 4, 6), R("P16"), R("RR"), False, False)
         for i in (1, 3, 4):
@@ -465,37 +518,47 @@ def rank_program(g, core, T, topo):
         if not last:
             mm(R("p7", 0, 1), R("ONE"), R("HN", 0, 1), True, False)
             mm(R("p7", 0, 1), R("ONE"), R("HN", 1, 2), False, True)
+        if t:
+            cp(R("KH"), R("p6", 0, 2))
+            act(R("O"), IND(R("NW%d" % t), R("KH")))
         for b in range(2):
             ts(R("YL", 8 * b, 8 * b + 8), R("M8"), R("p1", b, b + 1), A.mult)
         act(R("YS", 128, 256), IND(R("Y"), R("YL", 8, 16)))
         cp(R("YS", 0, 128), IND(R("Y"), R("YL", 0, 8)))
+        fill()
         for b in range(2):
-            mm(R("p3", b, b + 1), R("YS", 128 * b, 128 * b + 128), R("WB"))
-        cp(R("KH"), R("p2", 0, 2))
+            mm(R("p3", b, b + 1), R("ID"), R("C5"), True, False)
+            mm(R("p3", b, b + 1), R("YS", 128 * b, 128 * b + 128), R("WB"), False, True)
         if t:
-            act(R("O"), IND(R("NW%d" % t), R("KH")))
-        cp(R("SI"), R("p3", 0, 2))
-        op("v", lambda: V.tensor_scalar(T.UU[:], T.SI[:], 4095, None, A.bitwise_and), [R("UU")], [R("SI")])
-        ts(R("VV"), R("UU"), -2912.0, A.add)
+            tt(R("OX", 0, 128), IND(R("O"), R("LX", 0, 8)), R("EM", 0, 128), A.mult)
+        ts(R("SI"), R("p3", 0, 2), 1.0 / 4096, A.mult, -(2047.5 + 592) / 4096, A.add)
+        fill()
         for b in range(2):
-            ts(R("PP", b, b + 1), R("VV", b, b + 1), 7008.0, A.add, R("VV", b, b + 1), A.mult)
-        op("v", lambda: V.tensor_scalar(T.N0[:], T.PP[:], 5, 4095, A.arith_shift_right, A.bitwise_and), [R("N0")], [R("PP")])
+            ts(R("VV", b, b + 1), R("SI", b, b + 1), -4096.0, A.mult, R("p3", b, b + 1), A.add)
+        fill()
+        tt(R("PP"), R("VV"), R("VV"), A.mult)
+        fill()
+        bits(R("N0"), R("PP"), 5, A.arith_shift_right, 4095, A.bitwise_and)
+        fill()
         ts(R("NO"), R("N0"), R("CC"), A.add)
+        fill()
         look("E", 0, 32, R("NO"))
-        for h in range(2):
-            act(R("TG", 256 * h, 256 * h + 256), IND(R("TW"), R("E", 16 * h, 16 * h + 16)))
+        fill()
+        act(R("KY", 256, 512), IND(R("SC"), R("E", 16, 32)))
+        cp(R("KY", 0, 256), IND(R("SC"), R("E", 0, 16)))
+        if t:
+            tt(R("OX", 128, 256), IND(R("O"), R("LX", 8, 16)), R("EM", 128, 256), A.mult)
         mm(R("p4", 64, 96), R("CA"), R("O"))
         mm(R("p4", 96, 128), R("CBB"), R("O"))
-        if t:
-            tt(R("OX"), IND(R("O"), R("LX")), R("EM"), A.mult)
         for b in range(2):
             mm(R("p5", 4 * b + 2, 4 * b + 4), R("OX", 128 * b, 128 * b + 128), R("CB", 0, 2))
             mm(R("p5", 4 * b + 10, 4 * b + 12), R("OX", 128 * b, 128 * b + 128), R("CB", 4 + 4 * b, 6 + 4 * b))
         for h in range(2):
-            tt(R("KY", 256 * h, 256 * h + 256), IND(R("SC"), R("E", 16 * h, 16 * h + 16)), R("TG", 256 * h, 256 * h + 256), A.add)
             scan(R("KS", 256 * h, 256 * h + 256), R("KD"), R("KY", 256 * h, 256 * h + 256), 0.0, A.add, A.max)
         cp(R("KI"), R("KS", 15, 512, 16))
+        fill()
         tt(R("F"), R("KS", 15, 512, 16), R("KI"), A.subtract)
+        fill()
         mm(R("p4", 0, 32), R("CA"), R("F"))
         mm(R("p4", 32, 64), R("CBB"), R("F"))
         for b in range(2):
@@ -503,22 +566,28 @@ def rank_program(g, core, T, topo):
             mm(R("p5", 4 * b, 4 * b + 2), R("FX", 128 * b, 128 * b + 128), R("CB", 0, 2))
             mm(R("p5", 4 * b + 8, 4 * b + 10), R("FX", 128 * b, 128 * b + 128), R("CB", 2 + 4 * b, 4 + 4 * b))
         ts(R("NB"), R("p4", 0, 128), 0.5, A.max)
-        ac(R("LS"), R("p5", 0, 16))
-        op("v", lambda: V.tensor_scalar(T.NI[:], T.N0[:], T.CC[:, 0:1], None, A.add), [R("NI")], [R("N0"), R("CC")])
+        fill()
+        ts(R("NI"), R("N0"), R("CC"), A.add)
 
         def wrapped():
-            op("v", lambda: V.tensor_scalar(T.NJ[:], T.NI[:], 4095, None, A.bitwise_and), [R("NJ")], [R("NI")])
+            bits(R("NJ"), R("NI"), 4095, A.bitwise_and)
             cp(R("ME" if last else mst, 32, 34), R("NJ"))
         if last:
             wrapped()
             ac(R("ME", 44, 46), R("p2", 8, 10))
             send("ME", MW, [((rank - 4) % N, "HE", "he")])
+        fill()
         for i in range(8):
-            ts(R("EQ", 128 * i, 128 * i + 128), R("NB"), R("LS", i, i + 1), A.is_equal)
+            ts(R("EQ", 128 * i, 128 * i + 128), R("NB"), R("p5", i, i + 1), A.is_equal, R("W2", i // 4, i // 4 + 1), A.mult)
+        ac(R("LS", 0, 8), R("p5", 0, 8))
+        act(R("LS", 8, 16), R("p5", 8, 16), bias=1.75)
+        for b in range(2):
+            for nm in range(4):
+                mm(R("p6", 32 + 64 * b + 16 * nm, 48 + 64 * b + 16 * nm), R("TD", 128 * (nm % 2), 128 * (nm % 2) + 128), R("O" if nm > 1 else "F", 16 * b, 16 * b + 16))
         if not last:
             ac(R(mst, 34, 40), R("p2", 2, 8))
             ac(R(mst, 44, 46), R("p2", 8, 10))
-            ts(R("CC"), R("p7", 0, 1), -1.0, A.mult, 256.0, A.add)
+            ts(R("CC"), R("p7", 0, 1), -1.0, A.mult, 256.0 + 1336, A.add)
         scan(R("HS"), R("HD"), R("EQ"), 0.0, A.mult, A.add)
         cp(R("SU", 0, 8, 2), R("LS", 1, 8, 2))
         cp(R("SU", 1, 8, 2), R("LS", 0, 8, 2))
@@ -527,52 +596,59 @@ def rank_program(g, core, T, topo):
         act(R("ST"), IND(R("SC"), R("SU")))
         for b in range(2):
             red(R("RM", b, b + 1), R("HS", 512 * b + 127, 512 * b + 512, 128), A.max)
-        tt(R("OK"), R("RM"), R("THR"), A.is_lt)
-        for b in range(2):
-            ts(R("TT", 4 * b, 4 * b + 4), R("LS", 8 + 4 * b, 12 + 4 * b), R("OK", b, b + 1), A.mult)
-        for b in range(2):
-            if not last:
-                ac(R("DM", 16 * b, 16 * b + 16), R("E16"), R("OK", b, b + 1))
-            ts(R(mst, 40 + 2 * b, 42 + 2 * b), R("LS", 4 * b, 4 * b + 2), R("OK", b, b + 1), A.mult, -1.0, A.add)
         if last:
+            ts(R("OK"), R("RM"), 1.75, A.is_lt)
+            fill()
+            for b in range(2):
+                ts(R(mst, 40 + 2 * b, 42 + 2 * b), R("LS", 4 * b, 4 * b + 2), R("OK", b, b + 1), A.mult, -1.0, A.add)
             send(mst, MW, dests(t, rank), True)
+        for b in range(2):
+            ts(R("TT", 4 * b, 4 * b + 4), R("LS", 8 + 4 * b, 12 + 4 * b), R("RM", b, b + 1), A.max, 1.75, A.min)
+        if last:
+            fill()
         else:
-            mm(R("p6", 0, 32), R("BO"), R("DM"))
+            ts(R("OK"), R("RM"), 1.75, A.is_lt)
         tt(R("DF"), R("TT"), R("DT"), A.add)
-        cp(R("DU"), R("DF"))
+        fill()
+        if not last:
+            for b in range(2):
+                ac(R("DM", 16 * b, 16 * b + 16), R("E16"), R("OK", b, b + 1))
+            mm(R("p3", 32, 64), R("BO"), R("DM"))
+        ts(R("DU"), R("DF"), -1.75, A.add, 32768.0, A.mult)
+        fill()
         if not last:
             scatter(R("Z"), R("DU"), R("ZT"))
+            for b in range(2):
+                ts(R(mst, 40 + 2 * b, 42 + 2 * b), R("LS", 4 * b, 4 * b + 2), R("OK", b, b + 1), A.mult, -1.0, A.add)
             wrapped()
-            tt(R(mst, 0, 32), R("p6", 0, 32), R("F"), A.mult)
+            tt(R(mst, 0, 32), R("p3", 32, 64), R("F"), A.mult)
             send(mst, MW, dests(t, rank), True)
-        scatter(R("SC"), R("DU"), R("ST"))
+        tt(R("SN"), R("p6", 32, 160), R("ST"), A.add)
+        scatter(R("SC"), R("DU"), R("SN"))
+        fill(len(fillers))
 
     dma("y", T.ys[:], T.SC[15:128:16, 1:2049], [], [("SC", 1, 2049)])
     arrive("HE", "he", width(1))
-    for v in range(5):
-        m = "HM%d" % v if v else "MS0"
-        if v:
-            arrive(m, "h%d" % v, width(1 if v == 4 else len(dests(v, 0)) - 1))
-        e = "HE" if v == 4 else m
+    for b in range(2):
+        k = R("HE", 44 + b, 45 + b)
+        ts(R("KE", 32 * b, 32 * b + 32), R("IK"), k, A.not_equal)
+        ts(R("HV", b, 64, 2), R("IK"), k, A.is_equal, R("HE", 32 + b, 33 + b), A.mult)
+    for b in range(2):
+        tt(R("OUT", b, 64, 2), R("OUT", b, 64, 2), R("KE", 32 * b, 32 * b + 32), A.mult)
+    tt(R("OUT", 0, 64), R("OUT", 0, 64), R("HV", 0, 64), A.add)
+    dma("s", T.yk[:], T.OUT[:, 0:64], [], [("OUT", 0, 64)])
+    for f in range(2):
         for b in range(2):
-            k = R(e, 44 + b, 45 + b)
-            ts(R("KE"), R("IK"), k, A.not_equal)
-            tt(R("OUT", b, 192, 2), R("OUT", b, 192, 2), R("KE"), A.mult)
-            ts(R("HV", 96 * b, 96 * b + 32), R("IK", 0, 32), k, A.is_equal, R(e, 32 + b, 33 + b), A.mult)
-            if v == 4:
-                tt(R("OUT", b, 64, 2), R("OUT", b, 64, 2), R("HV", 96 * b, 96 * b + 32), A.add)
-        if v == 4:
-            dma("s", T.yk[:], T.OUT[:, 0:64], [], [("OUT", 0, 64)])
+            o = R("OF", 64 * f + b, 64 * f + 64, 2)
+            tt(o, o, R("KE", 32 * b, 32 * b + 32), A.mult)
+    arrive("HM4", "h4", width(1))
+    for f in range(2):
         for b in range(2):
-            k = R(e, 44 + b, 45 + b)
-            for f in (1, 2):
-                ts(R("HV", 96 * b + 32 * f, 96 * b + 32 * f + 32), R("IK", 0, 32), k, A.is_equal, R(m, 39 + 2 * b + f, 40 + 2 * b + f), A.mult)
-            if v == 4:
-                tt(R("OUT", 64 + b, 192, 2), R("OUT", 64 + b, 192, 2), R("HV", 96 * b + 32, 96 * b + 96), A.add)
-            else:
-                tt(R("OUT", b, 192, 2), R("OUT", b, 192, 2), R("HV", 96 * b, 96 * b + 96), A.add)
-    dma("y", T.ya[:], T.OUT[:, 64:128], [], [("OUT", 64, 128)])
-    dma("s", T.yb[:], T.OUT[:, 128:192], [], [("OUT", 128, 192)])
+            ts(R("HV", 64 * f + b, 64 * f + 64, 2), R("IK"), R("HE", 44 + b, 45 + b), A.is_equal, R("HM4", 40 + 2 * b + f, 41 + 2 * b + f), A.mult)
+    for f, y in enumerate(("ya", "yb")):
+        o = R("OF", 64 * f, 64 * f + 64)
+        tt(o, o, R("HV", 64 * f, 64 * f + 64), A.add)
+        dma("ys"[f], T[y][:], T.OF[:, 64 * f:64 * f + 64], [], [("OF", 64 * f, 64 * f + 64)])
     for i in range(st["dma"]):
         need("y", ("d%d" % i, 16))
     g.wait_ge(T.sem["loc"], st["loc"])

from concourse.bass import DstId, RemoteDMATransfer
from concourse.mybir import AluOpType as A, AxisListType, ActivationFunctionType as AF

SB = {
    "bk": (5696, "int32"), "trs": (2048, "bfloat16"), "sgi": (128, "int32"), "kmi": (64, "int32"), "wti": (8, "int32"),
    "Z": (2192, "bfloat16"), "SC": (2184, "float32"), "SF": (2048, "float32"),
    "IOS": (2048, "float32"), "HI": (2048, "bfloat16"), "LO": (2048, "bfloat16"),
    "sgu": (128, "uint16"), "Kp": (64, "uint16"), "kmf": (64, "float32"), "KX": (512, "float32"),
    "LP": (128, "uint16"), "E": (32, "uint16"), "NO": (2, "uint16"), "YL": (16, "uint16"), "KH": (2, "uint16"),
    "SU": (8, "uint16"), "DU": (8, "uint16"), "MO": (32, "uint16"),
    "GR": (16384, "bfloat16"), "Y": (16400, "bfloat16"), "GP": (2048, "bfloat16"), "YP": (2048, "bfloat16"),
    "Y0": (32, "bfloat16"), "CM": (1024, "bfloat16"), "CP": (128, "bfloat16"), "KV": (64, "float32"), "KT": (64, "float32"),
    "RR": (2, "bfloat16"), "HN": (2, "bfloat16"), "YS": (256, "bfloat16"), "SI": (2, "int32"), "C5": (1, "bfloat16"),
    "VV": (2, "float32"), "PP": (2, "int32"), "N0": (2, "int32"),
    "NI": (2, "int32"), "NJ": (2, "int32"), "CC": (1, "float32"), "SN": (128, "float32"), "KY": (512, "float32"), "KS": (512, "float32"),
    "KI": (32, "int32"), "F": (32, "bfloat16"), "FX": (256, "bfloat16"), "O": (32, "bfloat16"), "OX": (256, "bfloat16"),
    "NB": (128, "float16"), "LS": (16, "float32"), "EQ": (1024, "bfloat16"), "HS": (1024, "bfloat16"), "RM": (2, "float32"), "OK": (2, "float32"),
    "TT": (8, "float32"), "DF": (8, "float32"), "ZT": (128, "bfloat16"), "ST": (128, "float32"), "DM": (32, "bfloat16"),
    "OUT": (128, "float32"), "KE": (64, "float32"), "HV": (128, "float32"), "AV": (2, "float32"), "AI": (192, "int32"), "OF": (128, "float32"),
    "D0": (2048, "bfloat16"), "KD": (256, "float32"), "HD": (1024, "bfloat16"), "IO": (128, "float32"), "IG": (128, "float32"), "IP": (128, "float32"),
    "PI": (8, "int32"), "PF": (4, "float32"), "E16": (16, "float32"), "BO": (128, "bfloat16"), "BF4": (512, "float32"), "ID": (128, "bfloat16"), "P1": (128, "bfloat16"),
    "P16": (128, "bfloat16"), "PD": (256, "bfloat16"), "G8": (8, "bfloat16"), "M8": (8, "float32"), "SG": (128, "bfloat16"), "EM": (256, "bfloat16"),
    "EX": (128, "float32"), "CF": (20, "float32"), "CB": (16, "bfloat16"), "CA": (128, "bfloat16"), "CBB": (128, "bfloat16"), "ONE": (128, "bfloat16"),
    "LC": (64, "uint16"), "LX": (16, "uint16"), "LK": (32, "uint16"), "L0": (8, "uint16"), "LT": (96, "float32"),
    "T32": (32, "float32"), "Z32": (32, "float32"), "Q32": (32, "float32"), "DT": (8, "float32"), "BS1": (10, "bfloat16"), "BS2": (10, "bfloat16"),
    "TD": (256, "bfloat16"), "W2": (2, "float32"), "DH": (128, "bfloat16"), "DL": (128, "bfloat16"), "KC": (1, "float32"), "WB": (1, "bfloat16"), "IK": (32, "float32"),
}
MW = 48
SCRATCH = {}
PART = {}
for _n in SB:
    SCRATCH[_n] = ("sbuf", [128, SB[_n][0]], SB[_n][1])
    PART[_n] = (_n, 0, SB[_n][0])


def _parts(buf, names, w, dtype):
    SCRATCH[buf] = ("sbuf", [128, w * len(names)], dtype)
    for i, n in enumerate(names):
        PART[n] = (buf, w * i, w)


_parts("LBS", ["LB%d" % _t for _t in range(5)], 1024, "uint16")
_parts("KINS", ["KIN%d" % _t for _t in range(1, 5)], 64, "uint16")
_parts("NWS", ["NW%d" % _t for _t in range(1, 5)], 1056, "float32")
_parts("MSS", ["MS%d" % _t for _t in range(5)] + ["ME"], MW, "float32")
PART["MSS"] = ("MSS", 0, 6 * MW)
_parts("MGS", ["MG%d%d" % (_t, _v) for _t in range(1, 5) for _v in range(_t)], MW, "float32")
_parts("HMS", ["HM%d" % _v for _v in range(1, 5)] + ["HE"], MW, "float32")
for _b in range(8):
    SCRATCH["p%d" % _b] = ("psum", [128, 512], "float32")
    PART["p%d" % _b] = ("p%d" % _b, 0, 512)
SEMAPHORES = ["cv", "cs", "ct", "cg", "loc"] + ["d%d" % _i for _i in range(16)] + ["k%d" % _i for _i in range(1, 5)] + \
    ["m%d%d" % (_t, _v) for _t in range(1, 5) for _v in range(_t)] + ["h%d" % _v for _v in range(1, 5)] + ["he"]

SCH = [4, 4, 4, 4, 4, 3, 1]
VCH = [3, 3, 2]
PLAN = ["g0", "S0", "V0", "g1", "S1", "V1", "S2", "pg", "g2", "L0", "L1", "V2", "S3", "L2", "L3", "S4", "ps", "S5", "S6"]
NP = 3


def rank_program(g, core, T, topo):
    rank = T.rank_of(core)
    if rank is None:
        return
    N = len(T.cores)
    QU = {"v": g.vector, "s": g.scalar, "t": g.tensor, "g": g, "y": g.sync}
    SEM = {"v": "cv", "s": "cs", "t": "ct", "g": "cg"}
    cnt = {"cv": 0, "cs": 0, "ct": 0, "cg": 0}
    known = {q: {} for q in QU}
    vcs = {}
    acc = {}
    st = {"dma": 0, "loc": 0}

    def need(q, tok):
        sem, val = tok
        if known[q].get(sem, 0) >= val:
            return
        QU[q].wait_ge(T.sem[sem], val)
        kq = known[q]
        for s2, v2 in vcs.get(tok, {}).items():
            if kq.get(s2, 0) < v2:
                kq[s2] = v2
        kq[sem] = max(val, kq.get(sem, 0))

    def deps(q, outs, ins):
        ds = {}
        for w, regs in ((True, outs), (False, ins)):
            for (nm, lo, hi, sp) in regs:
                ps = nm[0] == "p"
                for (l2, h2, w2, q2, tok, s2) in acc.get(nm, ()):
                    if ps and (q2 != q):
                        hit = True
                    elif ps and q == "t":
                        hit = False
                    else:
                        hit = (w or w2) and l2 < hi and lo < h2 and not (sp > 1 and sp == s2 and (lo - l2) % sp)
                    if hit:
                        ds[tok[0]] = max(ds.get(tok[0], 0), tok[1])
        own = SEM.get(q)
        for sem in sorted(ds, key=lambda s: (s == own, s)):
            need(q, (sem, ds[sem]))

    def record(q, tok, outs, ins):
        v = dict(known[q])
        v[tok[0]] = tok[1]
        vcs[tok] = v
        for w, regs in ((True, outs), (False, ins)):
            for (nm, lo, hi, sp) in regs:
                old = acc.get(nm, [])

                def inside(r):
                    return lo <= r[0] and r[1] <= hi and (sp == 1 or (sp == r[5] and (lo - r[0]) % sp == 0))
                if w and nm[0] != "p":
                    old = [r for r in old if not inside(r)]
                else:
                    old = [r for r in old if not (r[3] == q and r[2] == w and inside(r) and r[4][0] == tok[0])]
                old.append((lo, hi, w, q, tok, sp))
                acc[nm] = old

    def R(nm, lo=0, hi=None, step=1):
        nm, off, wd = PART[nm]
        lo, hi = lo + off, off + (wd if hi is None else hi)
        return (T[nm][:, lo:hi] if step == 1 else T[nm][:, lo:hi:step], [(nm, lo, hi, step)])

    def IND(win, off):
        return (win[0].indirect(off[0]), win[1] + off[1])

    def reg(x):
        return x[1] if isinstance(x, tuple) else []

    def ap(x):
        return x[0] if isinstance(x, tuple) else x

    def op(q, fn, outs, ins):
        o = [r for x in outs for r in reg(x)]
        i = [r for x in ins for r in reg(x)]
        deps(q, o, i)
        sem = SEM[q]
        cnt[sem] += 1
        fn().then_inc(T.sem[sem], 1)
        record(q, (sem, cnt[sem]), o, i)

    V, S, PE = g.vector, g.scalar, g.tensor

    def cp(out, in_):
        op("v", lambda: V.tensor_copy(ap(out), ap(in_)), [out], [in_])

    def scatter(win, off, in_):
        op("v", lambda: V.tensor_copy(win[0].indirect(off[0]), ap(in_)), [win], [in_, off])

    def tt(out, a, b, o):
        op("v", lambda: V.tensor_tensor(ap(out), ap(a), ap(b), o), [out], [a, b])

    def ts(out, a, s1, o1, s2=None, o2=None):
        if o2 is None:
            op("v", lambda: V.tensor_scalar(ap(out), ap(a), ap(s1), None, o1), [out], [a, s1])
        else:
            op("v", lambda: V.tensor_scalar(ap(out), ap(a), ap(s1), ap(s2), o1, o2), [out], [a, s1, s2])

    def bits(out, a, s1, o1, s2=None, o2=None):
        if o2 is None:
            op("v", lambda: V.tensor_scalar(ap(out), ap(a), s1, None, o1), [out], [a])
        else:
            op("v", lambda: V.tensor_scalar(ap(out), ap(a), s1, s2, o1, o2), [out], [a])

    def ms(out, c):
        op("v", lambda: V.memset(ap(out), c), [out], [])

    def red(out, a, o):
        op("v", lambda: V.tensor_reduce(ap(out), ap(a), AxisListType.X, o), [out], [a])

    def scan(out, a, b, init, o1, o2):
        op("v", lambda: V.tensor_tensor_scan(ap(out), ap(a), ap(b), init, o1, o2), [out], [a, b])

    def act(out, a, **kw):
        d = {k: ap(x) for k, x in kw.items()}
        f = AF.Identity if "bias" in kw else AF.Copy
        op("s", lambda: S.activation(ap(out), ap(a), f, **d), [out], [a] + list(kw.values()))

    def ac(out, a, scale=1.0, bias=None):
        if bias is None:
            act(out, a, scale=scale)
        else:
            act(out, a, scale=scale, bias=bias)

    def mm(out, l, r, start=True, stop=True):
        op("t", lambda: PE.matmul(ap(out), ap(l), ap(r), start, stop), [out], [l, r])

    def iota(out, pat, base=0, cm=0):
        op("g", lambda: g.iota(ap(out), pat, base, cm, allow_small_or_imprecise_dtypes=True), [out], [])

    def dma(q, oap, iap, outs, ins):
        outs, ins = [x + (1,) for x in outs], [x + (1,) for x in ins]
        deps(q, outs, ins)
        sem = "d%d" % st["dma"]
        st["dma"] += 1
        QU[q].dma_start(oap, iap).then_inc(T.sem[sem], 16)
        record(q, (sem, 16), outs, ins)

    def send(src, ws, dsts, first=False):
        deps("g", [], R(src, 0, ws)[1])
        if first:
            send(src, ws, dsts[:1])
            if len(dsts) > 1:
                send(src, ws, dsts[1:])
            return
        k = 1
        while k < len(dsts):
            k *= 2
        tr = []
        for n, (r2, buf, sem) in enumerate(dsts):
            c2 = T.cores[r2]
            en = topo.engines(core, c2)
            w = max(1, len(en) // k)
            m = 0
            for e in en[n * w:(n + 1) * w]:
                m |= 1 << e
            rid, pid, _se = topo.addr(c2)
            tr.append(RemoteDMATransfer(dst_ids=[DstId(rid=rid, pnc=pid)], dma_engine_mask=m, remote_sem=T.sem[sem], src=R(src)[0], dst=R(buf)[0]))
            st["loc"] += w
        g.remote_dma_fused(tr, local_sem=T.sem["loc"])

    def width(n):
        k = 1
        while k < n:
            k *= 2
        return max(1, len(topo.engines(T.cores[(rank + 1) % N], core)) // k)

    def arrive(buf, sem, val):
        (nm, lo, hi, _sp), = R(buf)[1]
        acc.setdefault(nm, []).append((lo, hi, True, "r", (sem, val), 1))
        vcs[(sem, val)] = {sem: val}

    def dests(v, q):
        r = (q - v) % N
        d = [((r + t) % N, "MG%d%d" % (t, v), "m%d%d" % (t, v)) for t in range(v + 1, 5)]
        if v:
            d.append((r, "HM%d" % v, "h%d" % v))
        return d

    dma("s", T.sgi[:], T.sg0[:], [("sgi", 0, 128)], [])
    dma("s", T.kmi[:], T.km0[:], [("kmi", 0, 64)], [])
    dma("s", T.wti[:, 0:1], T.wt[:], [("wti", 0, 1)], [])
    dma("y", T.trs[:], T.tru[:], [("trs", 0, 2048)], [])
    dma("y", T.bk[:, 0:4096], T.book[:], [("bk", 0, 4096)], [])
    dma("y", T.bk[:, 4096:5696], T.book[:, 0:1600], [("bk", 4096, 5696)], [])

    op("g", lambda: g.iota(T.PI[:, 0:1], [[0, 1]], 0, 1), [R("PI", 0, 1)], [])
    iota(R("IO"), [[1, 128]])
    iota(R("IG"), [[1, 8], [0, 16]])
    iota(R("LT", 64, 96), [[32, 2], [1, 2], [0, 8]])
    iota(R("LT", 0, 64), [[1, 32], [0, 2]])
    iota(R("IP"), [[1, 8], [8, 4], [32, 4]])
    iota(R("IK"), [[1, 32]])
    iota(R("HI"), [[1, 64], [0, 32]])
    iota(R("LO"), [[0, 64], [1, 32]])
    iota(R("IOS"), [[1, 2048]])
    ms(R("D0"), 0.0)
    bits(R("PI", 1, 2), R("PI", 0, 1), 15, A.bitwise_and)
    bits(R("PI", 2, 3), R("PI", 0, 1), 4, A.arith_shift_right)
    bits(R("PI", 3, 4), R("PI", 0, 1), 31, A.bitwise_and)
    cp(R("PF", 0, 4), R("PI", 0, 4))
    ts(R("E16"), R("IO", 0, 16), R("PF", 1, 2), A.is_equal)
    ts(R("ID"), R("IO"), R("PF", 0, 1), A.is_equal)
    ts(R("BO"), R("IG"), R("PF", 2, 3), A.is_equal)
    ts(R("LT", 64, 96), R("LT", 64, 96), R("PF", 1, 2), A.add, R("PF", 1, 2), A.add)
    cp(R("LK"), R("LT", 64, 96))
    for i in range(4):
        ts(R("BF4", 128 * i, 128 * i + 128), R("IG"), R("PF", 2, 3), A.is_equal)
    ms(R("SG"), 0.0)
    ms(R("TD"), 0.0)
    for i in range(4):
        ac(R("SG", i, 128, 16), R("BO", i, 128, 16), 16.0 if i < 2 else -16.0)
    cp(R("LC"), R("LT", 0, 64))
    cp(R("sgu"), R("sgi"))
    cp(R("kmf"), R("kmi"))
    tt(R("KX"), IND(R("kmf"), R("LK")), R("BF4"), A.mult)
    for i in range(4):
        mm(R("p7", 16 * i, 16 * i + 16), R("KX", 128 * i, 128 * i + 128), R("E16"))
    ms(R("D0", 0, 2048, 16), 256.0)
    for kh in range(2):
        cp(R("Kp", kh, 64, 2), R("p7", 32 * kh, 32 * kh + 32))
    send("Kp", 64, [((rank + t) % N, "KIN%d" % t, "k%d" % t) for t in range(1, 5)])
    for t in range(1, 5):
        arrive("KIN%d" % t, "k%d" % t, width(4))
    ms(R("Z", 0, 1), 0.0)
    ms(R("Z", 2049, 2192), 0.0)

    def lin(*cols):
        prev = {c: f for c, _t, f in cols}
        for n in range(max(len(tm) for _c, tm, _f in cols)):
            for c, tm, _f in cols:
                if n < len(tm):
                    lane, val = tm[n]
                    if prev[c] is None:
                        ac(R("CF", c, c + 1), R("E16", lane, lane + 1), float(val))
                    else:
                        ac(R("CF", c, c + 1), R("E16", lane, lane + 1), float(val), R("CF", prev[c], prev[c] + 1))
                    prev[c] = c
    K = 1.0 / 32768
    lin((13, [(0, 1.0 / 64), (2, 1.0 / 64)], None), (14, [(1, 1.0 / 64), (3, 1.0 / 64)], None),
        (12, [(0, -63.0 / 128), (1, -63.0 / 128), (2, -63.0 / 128), (3, -63.0 / 128), (4, 0.25), (5, 0.25), (7, 0.25)], None),
        (0, [(0, 2048), (1, 64), (4, 4160), (5, 2)], None), (1, [(2, 2048), (3, 64), (4, 4160), (5, 2)], None),
        (10, [(0, 2048 * K), (1, 64 * K), (4, -4032 * K), (5, -2 * K), (7, -K)], None),
        (11, [(2, 2048 * K), (3, 64 * K), (4, -4032 * K), (5, -2 * K), (7, -K)], None),
        (15, [(0, 1), (2, -1)], None), (16, [(0, -1), (2, 1)], None), (17, [(1, 1), (3, -1)], None), (18, [(1, -1), (3, 1)], None))
    ac(R("DH"), R("ID"), R("CF", 13, 14))
    ac(R("DL"), R("ID"), R("CF", 14, 15))
    lin(*[(2 + q, [(5, -4 * q * K)], 10 + q % 2) for q in range(8)])
    ac(R("CB", 0, 10), R("CF", 0, 10))
    ac(R("CA"), R("BO"), R("CF", 0, 1))
    ac(R("CBB"), R("BO"), R("CF", 1, 2))
    for i in range(2):
        for l in (i, i + 2):
            for sg in range(2):
                ac(R("TD", 128 * sg + l, 128 * sg + 128, 16), R("BO", i, 128, 16), R("CF", 15 + 2 * i + sg, 16 + 2 * i + sg))
    cp(R("Z", 1, 1025), IND(R("trs"), R("sgu", 0, 64)))
    act(R("Z", 1025, 2049), IND(R("trs"), R("sgu", 64, 128)))
    for t in range(1, 5):
        iota(R("NW%d" % t), [[0, 1056]])
    ms(R("KD"), 1.0)
    ms(R("KD", 0, 256, 16), -1048576.0)
    ms(R("HD"), 8.0)
    ms(R("HD", 0, 1024, 32), 2.0 ** -93)
    ms(R("HD", 0, 1024, 128), 0.0)
    ts(R("P1"), R("IP"), R("PF", 0, 1), A.is_equal)
    ts(R("M8"), R("IO", 0, 8), R("PF", 2, 3), A.is_equal)
    ms(R("SC", 0, 1), 0.0)
    ms(R("SC", 2049, 2184), 0.0)
    ac(R("P16"), R("P1"), 16.0)
    ac(R("G8"), R("M8"))
    for i in range(4):
        mm(R("p%d" % i), R("SG"), R("Z", 1 + 512 * i, 513 + 512 * i), True, False)
        mm(R("p%d" % i), R("DH"), R("HI", 512 * i, 512 * i + 512), False, False)
        mm(R("p%d" % i), R("DL"), R("LO", 512 * i, 512 * i + 512), False, True)
    for i in range(4):
        act(R("SC", 1 + 512 * i, 513 + 512 * i), R("p%d" % i), bias=R("CF", 12, 13))
    ts(R("EX"), R("IG"), -16.0, A.mult)
    tt(R("EX"), R("EX"), R("IO"), A.add)
    ts(R("EX"), R("EX"), 32.0, A.mult, -1.0, A.add)
    ts(R("EX"), R("EX"), R("E16", 7, 8), A.mult, 1.0, A.add)
    for b in range(2):
        tt(R("EM", 128 * b, 128 * b + 128), R("EX"), R("BF4", 0, 128), A.mult)
    ts(R("Q32", 0, 2), R("IO", 0, 2), 16.0, A.mult, R("PF", 1, 2), A.add)
    for i in range(4):
        cp(R("L0", 2 * i, 2 * i + 2), R("Q32", 0, 2))
    ts(R("LX", 0, 8), R("IG", 0, 8), 0.0, A.mult, R("PF", 1, 2), A.add)
    ts(R("LX", 8, 16), R("IG", 0, 8), 16.0, A.add, R("PF", 1, 2), A.add)
    for i, (m1, c1, m2, c2) in enumerate([(32, 32, 1, 0), (32, 32, 1, 0), (512, 512, 0, 31), (32, 32, 0, 0), (0, 32, 0, 0)]):
        ts(R("BS1", 2 * i, 2 * i + 2), R("Q32", 0, 2), float(m1), A.mult, float(c1), A.add)
        ts(R("BS2", 2 * i, 2 * i + 2), R("Q32", 0, 2), float(m2), A.mult, float(c2), A.add)
    ms(R("T32"), 8.0)
    ms(R("Z32"), 0.0)
    scan(R("Q32"), R("T32"), R("Z32"), 2.0 ** -96, A.mult, A.add)
    for b in range(2):
        tt(R("T32", 16 * b, 16 * b + 16), R("Q32", 16 * b, 16 * b + 16), R("E16"), A.mult)
        red(R("W2", b, b + 1), R("T32", 16 * b, 16 * b + 16), A.add)
    ts(R("EX", 0, 1), R("PF", 1, 2), 8.0, A.mult, 2049.0, A.add)
    ts(R("DT"), R("IO", 0, 8), R("EX", 0, 1), A.add, K, A.mult)
    ts(R("KC"), R("PF", 3, 4), -32.0, A.add)
    cp(R("WB"), R("wti", 0, 1))
    ms(R("Y", 0, 16), 0.0)
    ms(R("O"), 0.0)
    ms(R("OX"), 0.0)
    ms(R("CC"), 1336.0)
    ms(R("C5"), 592.0)
    ms(R("ONE"), 1.0)
    ms(R("MSS"), 0.0)
    cp(R("OUT", 0, 64), R("kmi"))
    ms(R("OUT", 64, 128), -4097.0)

    def look(dst, c0, c1, lst):
        ts(R(dst, c0, c1), IND(R("bk"), lst), 1.0, A.add)
    for i in range(4):
        look("LB0", 256 * i, 256 * i + 256, R("Kp", 16 * i, 16 * i + 16))

    fillers = []

    def fill(n=1):
        for _i in range(n):
            if fillers:
                fillers.pop(0)()

    def go(f, *a):
        fillers.append(lambda: f(*a))

    def home(m):
        for b in range(2):
            go(ts, R("AV", b, b + 1), R(m, 40 + 2 * b, 41 + 2 * b), 4096.0, A.mult, R(m, 41 + 2 * b, 42 + 2 * b), A.add)
            go(ts, R("KE", 32 * b, 32 * b + 32), R("IK"), R(m, 44 + b, 45 + b), A.not_equal)
        for f in range(2):
            for b in range(2):
                o = R("OUT", 64 * f + b, 64 * f + 64, 2)
                go(tt, o, o, R("KE", 32 * b, 32 * b + 32), A.mult)
        for f in range(2):
            for b in range(2):
                go(ts, R("HV", 64 * f + b, 64 * f + 64, 2), R("IK"), R(m, 44 + b, 45 + b), A.is_equal, R("AV", b, b + 1) if f else R(m, 32 + b, 33 + b), A.mult)
        for f in range(2):
            o = R("OUT", 64 * f, 64 * f + 64)
            go(tt, o, o, R("HV", 64 * f, 64 * f + 64), A.add)

    def apart():
        go(ts, R("AI", 0, 64), R("OUT", 64, 128), 4097.0, A.add)
        go(bits, R("AI", 64, 128), R("AI", 0, 64), 12, A.arith_shift_right)
        go(bits, R("AI", 128, 192), R("AI", 0, 64), 4095, A.bitwise_and)
        go(ts, R("OF", 0, 64), R("AI", 64, 128), -1.0, A.add)
        go(ts, R("OF", 64, 128), R("AI", 128, 192), -1.0, A.add)

    sj, j0 = [], 0
    for n in SCH:
        sj.append((j0, j0 + n))
        j0 += n
    vj = []
    for n in VCH:
        vj.append((j0, j0 + n))
        j0 += n

    for t in range(5):
        L = "LB%d" % t
        mst = "MS%d" % t
        last = t == 4
        pend, pend0 = [], []

        def least(a, b):
            scan(R("Y", 16 + 512 * a, 16 + 512 * b), R("D0", 0, 512 * (b - a)), R("GR", 512 * a, 512 * b), 0.0, A.max, A.min)
            compare()
            pend0.append((a, b))

        def compare():
            first = pend0.pop(0) if pend0 else None
            if first:
                a, b = first
                cp(R("Y0", a, b), R("Y", 31 + 512 * a, 16 + 512 * b, 512))
            if pend:
                a, b = pend.pop(0)
                tt(R("CM", 32 * a, 32 * b), IND(R("Y0", 0, b), R("LC", 2 * a, 2 * b)), R("Y", 31 + 512 * a, 16 + 512 * b, 16), A.is_gt)
            if first:
                pend.append(first)

        def vec(w):
            if w in ("pg", "ps"):
                if w == "ps" and t:
                    scan(R("YP", 0, 512 * t), R("D0", 0, 512 * t), R("GP", 0, 512 * t), 0.0, A.max, A.min)
                return
            i = int(w[1])
            if w[0] == "L":
                if not last:
                    look("LB%d" % (t + 1), 256 * i, 256 * i + 256, R("KIN%d" % (t + 1), 16 * i, 16 * i + 16))
                return
            a, b = vj[i] if w[0] in "gV" else sj[i]
            if w[0] == "g":
                cp(R("GR", 512 * a, 512 * b), IND(R("Z"), R(L, 32 * a, 32 * b)))
                compare()
            else:
                least(a, b)
        for n, (a, b) in enumerate(sj):
            if n == 5 and t:
                act(R("GP", 0, 512 * t), IND(R("Z"), R("LP", 0, 32 * t)))
            act(R("GR", 512 * a, 512 * b), IND(R("Z"), R(L, 32 * a, 32 * b)))
            if n == NP - 1 and t:
                for w in PLAN[:PLAN.index("pg")]:
                    vec(w)
                for v in range(t):
                    arrive("MG%d%d" % (t, v), "m%d%d" % (t, v), width(1 if t == v + 1 else len(dests(v, 0)) - 1))
                for v in range(t):
                    cp(R("MO", 8 * v, 8 * v + 8), R("MG%d%d" % (t, v), 32, 40))
                    look("LP", 32 * v, 32 * v + 32, R("MO", 8 * v, 8 * v + 2))
                for v in range(t):
                    scatter(R("NW%d" % t), R("MO", 8 * v + 2, 8 * v + 4), R("MG%d%d" % (t, v), 0, 32))
        if not t:
            act(R("SF"), IND(R("IOS"), R("sgu")))
            dma("y", T.SC[15:128:16, 1:2049], T.SF[15:128:16, :], [("SC", 0, 2052)], [("SF", 0, 2048)])
        ac(R("PD", 128, 256), R("P1"), float(16 * (t - 31)))
        ac(R("PD", 0, 128), R("P1"), float(t - 31))
        for w in PLAN if not t else PLAN[PLAN.index("pg"):]:
            vec(w)
        compare()
        compare()
        if t:
            tt(R("CP", 0, 32 * t), IND(R("Y0"), R("L0", 0, 2 * t)), R("YP", 15, 512 * t, 16), A.is_gt)
        for v in range(t):
            scatter(R("CM"), R("MO", 8 * v + 6, 8 * v + 8), R("CP", 32 * v, 32 * v + 32))
        if t:
            if t > 1:
                arrive("HM%d" % (t - 1), "h%d" % (t - 1), width(len(dests(t - 1, 0)) - 1))
            home("HM%d" % (t - 1) if t > 1 else "MS0")
        if last:
            apart()
        mm(R("p1", 0, 2), R("ID"), R("BS1", 4, 6), True, False)
        mm(R("p1", 0, 2), R("ID"), R("BS2", 4, 6), False, False)
        mm(R("p2", 0, 10), R("ID"), R("BS1"), True, False)
        mm(R("p2", 0, 10), R("ID"), R("BS2"), False, False)
        mm(R("p6", 0, 2), R("ID"), R("BS1", 0, 2), True, False)
        mm(R("p6", 0, 2), R("ID"), R("BS2", 0, 2), False, False)
        for c in range(8):
            mm(R("p0", 8 * c, 8 * c + 8), R("CM", 128 * c, 128 * c + 128), R("G8"))
        for v in range(t):
            scatter(R("Y"), R("MO", 8 * v + 4, 8 * v + 6), R("YP", 512 * v + 15, 512 * v + 512, 16))
        ts(R("KV"), R("p0", 0, 64), 8.5, A.is_ge, R("KC"), A.mult)
        fill()
        op("v", lambda: V.transpose(T.KT[:], T.KV[:]), [R("KT")], [R("KV")])
        fill()
        for b in range(2):
            red(R("RR", b, b + 1), R("KT", 32 * b, 32 * b + 32), A.min)
        fill()
        mm(R("p1", 0, 2), R("P16"), R("RR"), False, False)
        mm(R("p6", 0, 2), R("P1"), R("RR"), False, True)
        ts(R("HN"), R("RR"), 0.0, A.is_equal)
        d1 = R("PD", 0, 128)
        d16 = R("PD", 128, 256)
        mm(R("p1", 0, 2), d16, R("HN"), False, True)
        for i in (1, 3, 4):
            mm(R("p2", 2 * i, 2 * i + 2), R("P1"), R("RR"), False, False)
        mm(R("p2", 4, 6), R("P16"), R("RR"), False, False)
        for i in (1, 3, 4):
            mm(R("p2", 2 * i, 2 * i + 2), d1, R("HN"), False, False)
        mm(R("p2", 4, 6), d16, R("HN"), False, True)
        if not last:
            mm(R("p7", 0, 1), R("ONE"), R("HN", 0, 1), True, False)
            mm(R("p7", 0, 1), R("ONE"), R("HN", 1, 2), False, True)
        if t:
            cp(R("KH"), R("p6", 0, 2))
            act(R("O"), IND(R("NW%d" % t), R("KH")))
        for b in range(2):
            ts(R("YL", 8 * b, 8 * b + 8), R("M8"), R("p1", b, b + 1), A.mult)
        act(R("YS", 128, 256), IND(R("Y"), R("YL", 8, 16)))
        cp(R("YS", 0, 128), IND(R("Y"), R("YL", 0, 8)))
        fill()
        for b in range(2):
            mm(R("p3", b, b + 1), R("ID"), R("C5"), True, False)
            mm(R("p3", b, b + 1), R("YS", 128 * b, 128 * b + 128), R("WB"), False, True)
        if t:
            tt(R("OX", 0, 128), IND(R("O"), R("LX", 0, 8)), R("EM", 0, 128), A.mult)
        ts(R("SI"), R("p3", 0, 2), 1.0 / 4096, A.mult, -(2047.5 + 592) / 4096, A.add)
        fill()
        for b in range(2):
            ts(R("VV", b, b + 1), R("SI", b, b + 1), -4096.0, A.mult, R("p3", b, b + 1), A.add)
        fill()
        tt(R("PP"), R("VV"), R("VV"), A.mult)
        fill()
        bits(R("N0"), R("PP"), 5, A.arith_shift_right, 4095, A.bitwise_and)
        fill()
        ts(R("NO"), R("N0"), R("CC"), A.add)
        fill()
        look("E", 0, 32, R("NO"))
        fill()
        act(R("KY", 256, 512), IND(R("SC"), R("E", 16, 32)))
        cp(R("KY", 0, 256), IND(R("SC"), R("E", 0, 16)))
        if t:
            tt(R("OX", 128, 256), IND(R("O"), R("LX", 8, 16)), R("EM", 128, 256), A.mult)
        mm(R("p4", 64, 96), R("CA"), R("O"))
        mm(R("p4", 96, 128), R("CBB"), R("O"))
        for b in range(2):
            mm(R("p5", 4 * b + 2, 4 * b + 4), R("OX", 128 * b, 128 * b + 128), R("CB", 0, 2))
            mm(R("p5", 4 * b + 10, 4 * b + 12), R("OX", 128 * b, 128 * b + 128), R("CB", 4 + 4 * b, 6 + 4 * b))
        for h in range(2):
            scan(R("KS", 256 * h, 256 * h + 256), R("KD"), R("KY", 256 * h, 256 * h + 256), 0.0, A.add, A.max)
        cp(R("KI"), R("KS", 15, 512, 16))
        fill()
        tt(R("F"), R("KS", 15, 512, 16), R("KI"), A.subtract)
        fill()
        mm(R("p4", 0, 32), R("CA"), R("F"))
        mm(R("p4", 32, 64), R("CBB"), R("F"))
        for b in range(2):
            tt(R("FX", 128 * b, 128 * b + 128), IND(R("F"), R("LX", 8 * b, 8 * b + 8)), R("EM", 128 * b, 128 * b + 128), A.mult)
            mm(R("p5", 4 * b, 4 * b + 2), R("FX", 128 * b, 128 * b + 128), R("CB", 0, 2))
            mm(R("p5", 4 * b + 8, 4 * b + 10), R("FX", 128 * b, 128 * b + 128), R("CB", 2 + 4 * b, 4 + 4 * b))
        ts(R("NB"), R("p4", 0, 128), 0.5, A.max)
        fill()
        ts(R("NI"), R("N0"), R("CC"), A.add)

        def wrapped():
            bits(R("NJ"), R("NI"), 4095, A.bitwise_and)
            cp(R("ME" if last else mst, 32, 34), R("NJ"))
        if last:
            wrapped()
            ac(R("ME", 44, 46), R("p2", 8, 10))
            send("ME", MW, [((rank - 4) % N, "HE", "he")])
        fill()
        for i in range(8):
            ts(R("EQ", 128 * i, 128 * i + 128), R("NB"), R("p5", i, i + 1), A.is_equal, R("W2", i // 4, i // 4 + 1), A.mult)
        ac(R("LS", 0, 8), R("p5", 0, 8))
        act(R("LS", 8, 16), R("p5", 8, 16), bias=1.75)
        for b in range(2):
            for nm in range(4):
                mm(R("p6", 32 + 64 * b + 16 * nm, 48 + 64 * b + 16 * nm), R("TD", 128 * (nm % 2), 128 * (nm % 2) + 128), R("O" if nm > 1 else "F", 16 * b, 16 * b + 16))
        if not last:
            ac(R(mst, 34, 40), R("p2", 2, 8))
            ac(R(mst, 44, 46), R("p2", 8, 10))
            ts(R("CC"), R("p7", 0, 1), -1.0, A.mult, 256.0 + 1336, A.add)
        scan(R("HS"), R("HD"), R("EQ"), 0.0, A.mult, A.add)
        cp(R("SU", 0, 8, 2), R("LS", 1, 8, 2))
        cp(R("SU", 1, 8, 2), R("LS", 0, 8, 2))
        if not last:
            act(R("ZT"), IND(R("Z"), R("SU")))
        act(R("ST"), IND(R("SC"), R("SU")))
        for b in range(2):
            red(R("RM", b, b + 1), R("HS", 512 * b + 127, 512 * b + 512, 128), A.max)
        if last:
            ts(R("OK"), R("RM"), 1.75, A.is_lt)
            fill()
            for b in range(2):
                ts(R(mst, 40 + 2 * b, 42 + 2 * b), R("LS", 4 * b, 4 * b + 2), R("OK", b, b + 1), A.mult, -1.0, A.add)
            send(mst, MW, dests(t, rank), True)
        for b in range(2):
            ts(R("TT", 4 * b, 4 * b + 4), R("LS", 8 + 4 * b, 12 + 4 * b), R("RM", b, b + 1), A.max, 1.75, A.min)
        if last:
            fill()
        else:
            ts(R("OK"), R("RM"), 1.75, A.is_lt)
        tt(R("DF"), R("TT"), R("DT"), A.add)
        fill()
        if not last:
            for b in range(2):
                ac(R("DM", 16 * b, 16 * b + 16), R("E16"), R("OK", b, b + 1))
            mm(R("p3", 32, 64), R("BO"), R("DM"))
        ts(R("DU"), R("DF"), -1.75, A.add, 32768.0, A.mult)
        fill()
        if not last:
            scatter(R("Z"), R("DU"), R("ZT"))
            for b in range(2):
                ts(R(mst, 40 + 2 * b, 42 + 2 * b), R("LS", 4 * b, 4 * b + 2), R("OK", b, b + 1), A.mult, -1.0, A.add)
            wrapped()
            tt(R(mst, 0, 32), R("p3", 32, 64), R("F"), A.mult)
            send(mst, MW, dests(t, rank), True)
        tt(R("SN"), R("p6", 32, 160), R("ST"), A.add)
        scatter(R("SC"), R("DU"), R("SN"))
        fill(len(fillers))

    dma("y", T.ys[:], T.SC[15:128:16, 1:2049], [], [("SC", 1, 2049)])
    arrive("HE", "he", width(1))
    for b in range(2):
        k = R("HE", 44 + b, 45 + b)
        ts(R("KE", 32 * b, 32 * b + 32), R("IK"), k, A.not_equal)
        ts(R("HV", b, 64, 2), R("IK"), k, A.is_equal, R("HE", 32 + b, 33 + b), A.mult)
    for b in range(2):
        tt(R("OUT", b, 64, 2), R("OUT", b, 64, 2), R("KE", 32 * b, 32 * b + 32), A.mult)
    tt(R("OUT", 0, 64), R("OUT", 0, 64), R("HV", 0, 64), A.add)
    dma("s", T.yk[:], T.OUT[:, 0:64], [], [("OUT", 0, 64)])
    for f in range(2):
        for b in range(2):
            o = R("OF", 64 * f + b, 64 * f + 64, 2)
            tt(o, o, R("KE", 32 * b, 32 * b + 32), A.mult)
    arrive("HM4", "h4", width(1))
    for f in range(2):
        for b in range(2):
            ts(R("HV", 64 * f + b, 64 * f + 64, 2), R("IK"), R("HE", 44 + b, 45 + b), A.is_equal, R("HM4", 40 + 2 * b + f, 41 + 2 * b + f), A.mult)
    for f, y in enumerate(("ya", "yb")):
        o = R("OF", 64 * f, 64 * f + 64)
        tt(o, o, R("HV", 64 * f, 64 * f + 64), A.add)
        dma("ys"[f], T[y][:], T.OF[:, 64 * f:64 * f + 64], [], [("OF", 64 * f, 64 * f + 64)])
    for i in range(st["dma"]):
        need("y", ("d%d" % i, 16))
    g.wait_ge(T.sem["loc"], st["loc"])
    need("g", ("cg", cnt["cg"]))
    for q, s in (("v", "cv"), ("s", "cs"), ("t", "ct")):
        need(q, (s, cnt[s]))
